import numpy as np, ml_dtypes
CORES = [2,3,42,43,82,83,122,123]
N = 8
import mx_ref
BF = ml_dtypes.bfloat16
def cols(t, e):
    v = np.concatenate([t.reshape(128, -1, 4), np.zeros((128, 1, 4), BF)], axis=1)
    return np.ascontiguousarray(v[:, e]).reshape(128, -1)
def cut(t, i, w=512):
    return t[:, w * i:w * i + w]
def f(rng, *shape):
    return mx_ref.flush((rng.standard_normal(shape, dtype=np.float32) * np.exp2(rng.integers(-2, 3, shape[:-1] + (1,)))).astype(BF))
def wide(rng, *shape, cols=0):
    v = rng.standard_normal(shape, dtype=np.float32) * np.exp2(rng.integers(-12, 13, shape)).astype(np.float32)
    if cols: v *= np.repeat(np.exp2(rng.integers(-cols, cols + 1, shape[:-2] + (1, shape[-1] // 4))) * (rng.random(shape[:-2] + (1, shape[-1] // 4)) > 0.0625), 4, axis=-1).astype(np.float32)
    return mx_ref.flush(v.astype(BF))
P, K, R, O = 512, 16, 4, 1
def bf(v):
    return mx_ref.flush(np.asarray(v, np.float32).astype(BF))
def same(v):
    t = np.zeros((128, 512), BF)
    t[:, :4] = v
    return np.stack([t] * N)
def setup_inputs(rng):
    return {"x": f(rng, N, 128, 4 * P), "u": same(f(rng, 128, 4)), "w": f(rng, N, 128, 512 * O)}
def setup_inputs_ties(rng):
    d = setup_inputs(rng)
    T = (P - K - 1) // 3
    H = T // 2
    shared = f(rng, 128, 4 * H)
    x = []
    for r in range(N):
        pool = np.concatenate([shared, f(rng, 128, 4 * (T + 1 - H))], axis=1)
        e = np.concatenate([np.repeat(np.arange(T), 3), np.full(P - 3 * T, T)])
        x.append(cols(pool, rng.permutation(e)))
    d["x"] = np.stack(x)
    d["u"] = bf(d["u"].astype(np.float32) * np.float32(256))
    return d
def setup_inputs_like(rng):
    d = setup_inputs(rng)
    at = rng.permutation(8)
    size = np.zeros(8)
    size[at] = np.exp2(-3.0 - np.arange(8) // 2)
    d["u"] = same(bf((1 + 0.25 * rng.random((128, 4))) * np.repeat(size, 16)[:, None]))
    side = rng.permutation(N) % 2
    x = []
    for r in range(N):
        c = rng.permutation(np.arange(P) % 8)
        h = np.where(c % 2 == side[r], 1.0, 0.75)
        on = np.repeat(np.arange(8)[:, None] == at[c][None, :], 16, axis=0) * h[None, :]
        x.append(bf((on[:, :, None] * (1 + 0.25 * rng.random((128, P, 4))) + 2.0 ** -8 * rng.standard_normal((128, P, 4))).reshape(128, 4 * P)))
    d["x"] = np.stack(x)
    return d
def setup_inputs_late(rng):
    d = setup_inputs(rng)
    half = (np.arange(128) < 64) ^ bool(rng.integers(0, 2))
    d["u"] = same(bf(2.0 ** 28 * (R - 1.5) * (1 + 0.25 * rng.random((128, 4))) * half[:, None]))
    x = []
    for r in range(N):
        late = rng.permutation(P) < rng.integers(2 * K, P // 2 + 1)
        v = np.where(half, 2.0 ** 22, 2.0 ** 26)[:, None] * np.where(late, -1.0, 1.0)[None, :]
        x.append(bf((v[:, :, None] * (1 + 0.25 * rng.random((128, P, 4)))).reshape(128, 4 * P)))
    d["x"] = np.stack(x)
    return d
def setup_inputs_low(rng):
    d = setup_inputs(rng)
    size = np.full((N, P), 2.0 ** 29)
    for r in range(N):
        e = 32 * int(rng.integers(0, P // 32)) + rng.permutation(32)[:K]
        size[r, e] = 2.0 ** 28
        size[r, e[:int(rng.integers(2, K // 2 + 1))]] = 0
    d["x"] = bf(np.repeat(size, 4, axis=1)[:, None, :] * (1.5 + 0.45 * rng.random((N, 128, 4 * P))))
    d["u"] = same(bf(-2.0 ** 29 * (1.5 + 0.45 * rng.random((128, 4)))))
    return d
def setup_inputs_spread(rng):
    d = setup_inputs(rng)
    d["x"] = wide(rng, N, 128, 4 * P, cols=6)
    d["u"] = same(bf(wide(rng, 128, 4).astype(np.float32) * np.float32(256)))
    return d
def check_inputs(d):
    b = []
    for k in ("x", "u", "w"):
        v = np.abs(d[k].astype(np.float32))
        if not (np.isfinite(v).all() and ((v == 0) | (v >= 2.0 ** -30) & (v <= 2.0 ** 30)).all()): b.append("a value of " + k)
    v = d["u"].astype(np.float32)
    if (v[:, :, 4:] != 0).any(): b.append("u has numbers behind its first column")
    if (v != v[:1]).any(): b.append("u isn't the same on all ranks")
    return b
def reference(x, u, w):
    X = [mx_ref.quantize(np.ascontiguousarray(x[r])) for r in range(N)]
    s = [mx_ref.matmul(mx_ref.quantize(np.ascontiguousarray(u[r])), X[r])[0] + np.float32(0.0) for r in range(N)]
    free = np.ones((N, P), bool)
    ch, se, y = np.zeros((N, R, K), np.float32), np.zeros((N, 1, P), np.float32), np.zeros((N, 128, O * R * 128), np.float32)
    M = []
    for b in range(R):
        best = []
        for r in range(N):
            e = np.argsort(np.where(free[r], -s[r], np.float32(np.inf)), kind="stable")[:K]
            free[r, e] = False
            ch[r, b] = e
            best.append(cols(x[r], e))
        M.append(mx_ref.quantize(np.ascontiguousarray(np.concatenate(best, axis=1))))
        if b < R - 1:
            for r in range(N):
                m = mx_ref.matmul(M[b], X[r]).max(axis=0) + np.float32(0.0)
                s[r] = s[r] - np.float32(0.25) * m
    for r in range(N):
        se[r, 0] = s[r]
        for o in range(O):
            q = mx_ref.quantize(np.ascontiguousarray(cut(w[r], o)))
            for b in range(R):
                i = (o * R + b) * 128
                y[r, :, i:i + 128] = mx_ref.matmul(q, M[b])
    return {"ch": ch, "se": se, "y": y}

@@ -1,0 +1,329 @@
+from concourse.bass import DstId, RemoteDMATransfer
+from concourse.mybir import dt, AluOpType, AxisListType, ActivationFunctionType
+
+R = 4
+COPY = ActivationFunctionType.Copy
+IDENT = ActivationFunctionType.Identity
+ABS = ActivationFunctionType.Abs
+RELU = ActivationFunctionType.Relu
+A = AluOpType
+BIG = 1e29
+
+
+def sb(n, d="float32"):
+    return ("sbuf", [128, n], d)
+
+
+F8, U8, BF = "float8_e4m3fn_x4", "uint8", "bfloat16"
+SCRATCH = {
+    "xt": sb(2048, BF), "ut": sb(512, BF), "wt": sb(512, BF),
+    "xq": sb(512, F8), "xs": sb(512, U8),
+    "pq": sb(512, F8), "pz": sb(512, U8),
+    "uq": sb(128, F8), "us": sb(128, U8), "vq": sb(128, F8), "vs": sb(128, U8), "wq": sb(128, F8), "ws": sb(128, U8),
+    "ip": sb(1, "int32"), "ir": sb(2, "int32"),
+    "rc": sb(4),
+    "ki": sb(32),
+    "k16": sb(32),
+    "kim": sb(32),
+    "mbig": sb(32),
+    "rb": sb(32),
+    "c4": sb(4), "jn": sb(4), "nj": sb(4),
+    "pm": sb(32), "po": sb(32, "uint16"),
+    "zo": sb(8, "uint16"),
+    "nq": sb(32), "z32": sb(32),
+    "B": sb(128 * R),
+    "Q": sb(128 * R),
+    "bm": sb(128 * R), "cmp": sb(640 * R, BF), "junk": sb(640 * R, BF), "jj": sb(128 * R), "lr": sb(4 * R),
+    "ab": sb(128 * R), "wv": sb(128 * R), "wj": sb(128 * R, BF), "wvt": sb(128 * R), "wjt": sb(128 * R, BF), "vc": sb(R),
+    "jcol": sb(R), "bv": sb(32 * R), "vt": sb(32 * R), "gg": sb(96 * R), "c2": sb(96 * R), "n2": sb(R), "w2": sb(32 * R),
+    "w2x": sb(80 * R), "lf": sb(R), "lb": sb(32 * R), "lt": sb(32 * R), "ind": sb(32 * R), "indt": sb(32 * R), "tt": sb(R),
+    "pen": sb(4 * R), "sm": sb(4 * R), "mm": sb(4 * R), "m25": sb(4 * R), "sc": sb(4 * R), "sb": sb(128), "sr": sb(128),
+    "yo": sb(512), "ps": ("psum", [128, 2048], "float32"), "py": ("psum", [128, 2048], "float32"),
+}
+for _b in range(R):
+    SCRATCH["of%d" % _b] = sb(2, "uint16")
+    SCRATCH["mq%d" % _b] = sb(128, F8)
+    SCRATCH["ms%d" % _b] = sb(128, U8)
+
+SEMAPHORES = ["sv", "sa", "st", "sg", "du", "dw", "dse", "loc"]
+SEMAPHORES += ["dx%d" % i for i in range(4)]
+SEMAPHORES += ["%s%d" % (n, b) for n in ("nq", "nz", "far", "dy", "dch") for b in range(R)]
+
+
+def mask_of(engines):
+    return sum(1 << e for e in engines)
+
+
+def rank_program(g, core, T, topo):
+    rank = T.rank_of(core)
+    if rank is None:
+        return
+    cores = list(T.cores)
+    chips = []
+    for c in cores:
+        if topo.chip(c) not in chips:
+            chips.append(topo.chip(c))
+    on = lambda ch: [r for r in range(len(cores)) if topo.chip(cores[r]) == ch]
+    at = chips.index(topo.chip(core))
+    pair = on(chips[at])
+    mate = [r for r in pair if r != rank]
+    ahead = on(chips[(at + 1) % len(chips)])
+    rest = [on(chips[(at + k) % len(chips)])[pair.index(rank)] for k in (3, 2)]
+    far_eng = topo.engines(core, cores[ahead[0]])
+    near_eng = [e for e in topo.engines(core, cores[mate[0]]) if e not in far_eng]
+    n_far = len(far_eng) * 2 * (len(ahead) + len(rest))
+
+    Q = {"v": g.vector, "a": g.scalar, "t": g.tensor, "g": g, "s": g.sync}
+    count = {"v": 0, "a": 0, "t": 0, "g": 0}
+    seen = {k: {} for k in Q}
+
+    def wait(q, deps):
+        need = {}
+        for d in deps:
+            for s, n in (d if isinstance(d, list) else [d]):
+                need[s] = max(need.get(s, 0), n)
+        for s, n in need.items():
+            if seen[q].get(s, 0) < n:
+                Q[q].wait_ge(T.sem[s], n)
+                seen[q][s] = n
+
+    def done(q, ins):
+        count[q] += 1
+        ins.then_inc(T.sem["s" + q], 1)
+        return ("s" + q, count[q])
+
+    def ts(out, in0, s1, op0, *deps, s2=None, op1=None):
+        wait("v", deps)
+        if op1 is None:
+            return done("v", g.vector.tensor_scalar(out, in0, s1, None, op0))
+        return done("v", g.vector.tensor_scalar(out, in0, s1, s2, op0, op1))
+
+    def tt(out, a, b, op, *deps):
+        wait("v", deps)
+        return done("v", g.vector.tensor_tensor(out, a, b, op))
+
+    def red(out, in_, op, *deps):
+        wait("v", deps)
+        return done("v", g.vector.tensor_reduce(out, in_, AxisListType.X, op))
+
+    def turn(out, in_, *deps):
+        wait("v", deps)
+        return done("v", g.vector.transpose(out, in_))
+
+    def vcopy(out, in_, *deps):
+        wait("v", deps)
+        return done("v", g.vector.tensor_copy(out, in_))
+
+    def fill(out, c):
+        return done("v", g.vector.memset(out, c))
+
+    def quant(q, s, x, *deps):
+        wait("v", deps)
+        return done("v", g.vector.quantize_mx(q, s, x))
+
+    def act(out, in_, func, *deps, **kw):
+        wait("a", deps)
+        return done("a", g.scalar.activation(out, in_, func, **kw))
+
+    def mm(out, lq, ls, rq, rs, *deps):
+        wait("t", deps)
+        return done("t", g.tensor.matmul_mx(out, lq, ls, rq, rs, True, True))
+
+    def load(q, out, in_, sem, *deps):
+        wait(q, deps)
+        Q[q].dma_start(out, in_).then_inc(T.sem[sem], 16)
+        return (sem, 16)
+
+    def send(view, *groups):
+        g.remote_dma_fused([
+            RemoteDMATransfer(dst_ids=[DstId(rid=topo.addr(cores[r])[0], pnc=topo.addr(cores[r])[1]) for r in to],
+                              dma_engine_mask=mask_of(eng), remote_sem=T.sem[arr], srcs=[view], dsts=[view for r in to])
+            for to, eng, arr in groups], local_sem=T.sem.loc)
+
+    lu = load("a", T.ut[:, 0:64], T.u[:, 0:64], "du")
+    lx = [load("s" if i % 2 == 0 else "a", T.xt[:, 512 * i:512 * i + 512], T.x[:, 512 * i:512 * i + 512], "dx%d" % i)
+          for i in range(4)]
+    lw = load("s", T.wt[:], T.w[:], "dw", lx[0])
+
+    iota = lambda out, pat, cm, **kw: done("g", g.iota(out, pat, 0, cm, **kw))
+    flag = {"allow_small_or_imprecise_dtypes": True}
+    k_zo = fill(T.zo[:], 0)
+    k_u = fill(T.ut[:, 64:512], 0.0)
+    k_ip = iota(T.ip[:], [[0, 1]], 1)
+    k_ki = iota(T.ki[:], [[1, 32]], 0, **flag)
+    k_16 = iota(T.k16[:], [[0, 2], [1, 16]], 0, **flag)
+    k_c4 = iota(T.c4[:], [[32, 4]], 0, **flag)
+    k_pm = iota(T.pm[:], [[32, 4], [128, 4], [16, 2]], 0, **flag)
+    k_nq = fill(T.nq[:], -0.25)
+    k_z = fill(T.z32[:], 0.0)
+    k_gg = fill(T.gg[:], -BIG)
+    a1 = ts(T.ir[:, 0:1], T.ip[:], 31, A.bitwise_and, k_ip)
+    a2 = ts(T.ir[:, 1:2], T.ip[:], 15, A.bitwise_and)
+    a3 = vcopy(T.rc[:, 3:4], T.ip[:])
+    k_rc = vcopy(T.rc[:, 0:2], T.ir[:], a1, a2)
+    ts(T.rc[:, 2:3], T.rc[:, 3:4], T.rc[:, 0:1], A.subtract, k_rc, a3, s2=1.0 / 32, op1=A.mult)
+    ts(T.kim[:], T.k16[:], T.rc[:, 0:1], A.subtract, k_16)
+    k_mb = ts(T.mbig[:], T.ki[:], T.rc[:, 0:1], A.is_ge, k_ki, s2=BIG, op1=A.mult)
+    ts(T.rb[:], T.z32[:], T.rc[:, 0:1], A.add, k_z)
+    k_po = ts(T.po[:], T.pm[:], T.rc[:, 1:2], A.add, k_pm)
+    k_jn = ts(T.jn[:], T.c4[:], T.rc[:, 0:1], A.add, k_c4)
+    k_con = ts(T.nj[:], T.jn[:], -1.0, A.mult, k_jn)
+
+    qu = quant(T.uq[:], T.us[:], T.ut[:], lu, k_u)
+    u1 = vcopy(T.vq[:].bitcast(dt.uint32), T.uq[:].bitcast(dt.uint32).indirect(T.zo[:, 0:8]), qu, k_zo)
+    u2 = act(T.vs[:], T.us[:].indirect(T.zo[:, 0:8]), COPY, qu, k_zo)
+    tq, qx = [], []
+    for i in range(4):
+        c = slice(128 * i, 128 * i + 128)
+        qx.append(quant(T.xq[:, c], T.xs[:, c], T.xt[:, 512 * i:512 * i + 512], lx[i]))
+    for i in range(4):
+        c = slice(128 * i, 128 * i + 128)
+        h = slice(32 * i, 32 * i + 32)
+        t = mm(T.ps[:, 512 * i:512 * i + 128], T.vq[:], T.vs[:], T.xq[:, c], T.xs[:, c], u1, u2, qx[i])
+        if i % 2 == 0:
+            tq.append(vcopy(T.Q[h, 0:128], T.ps[h, 512 * i:512 * i + 128], t))
+        else:
+            tq.append(act(T.Q[h, 0:128], T.ps[h, 512 * i:512 * i + 128], COPY, t))
+    tb = [turn(T.B[:, 0:128], T.Q[:, 0:128], *tq, k_con)] * 4
+    bank_free = list(tq)
+    y_todo = []
+    qw = perm = sc = None
+
+    def span(a, n):
+        return slice(32 * a, 32 * a + 32 * n)
+    moves = [(span(0, 2), span(2, 2), 0, 1), (span(2, 2), span(0, 2), 0, 0)]
+    for x, slot in ((1, 1), (3, 2)):
+        for a in range(4):
+            moves.append((span(a, 1), span(a ^ x, 1), slot, 1 if (a ^ x) > a else 0))
+
+    for b in range(R):
+        o = 128 * b
+        if b > 0:
+            tq = [turn(T.Q[:, o:o + 128], T.B[:, o:o + 128], *tb)]
+        bm = [act(T.bm[:, o + 32 * c:o + 32 * c + 32], T.mbig[:], IDENT, tb[c], k_mb,
+                  bias=T.B[:, o + 32 * c:o + 32 * c + 1]) for c in range(4)]
+        lr = []
+        for c in range(4):
+            s = T.B[:, o + 32 * c:o + 32 * c + 1]
+            w = 640 * b + 160 * c
+            d = []
+            if c > 0:
+                d.append(ts(T.cmp[:, w:w + 32 * c], T.Q[:, o:o + 32 * c], s, A.is_ge, tq, tb))
+            d.append(ts(T.cmp[:, w + 32 * c:w + 128], T.Q[:, o + 32 * c:o + 128], s, A.is_gt, tq, tb))
+            d.append(tt(T.cmp[:, w + 128:w + 160], T.Q[:, o + 32 * c:o + 32 * c + 32],
+                        T.bm[:, o + 32 * c:o + 32 * c + 32], A.is_equal, bm[c]))
+            lr.append(act(T.junk[:, w:w + 160], T.cmp[:, w:w + 160], COPY, d, accum_out=T.lr[:, 4 * b + c:4 * b + c + 1]))
+        cc = [slice(o + 32 * c, o + 32 * c + 32) for c in range(4)]
+        lc = [T.lr[:, 4 * b + c:4 * b + c + 1] for c in range(4)]
+        wv = [ts(T.wv[:, cc[c]], T.ki[:], lc[c], A.is_equal, lr[c], s2=T.B[:, o + 32 * c:o + 32 * c + 1], op1=A.mult)
+              for c in range(4)]
+        ab = [act(T.ab[:, cc[c]], T.ki[:], ABS, lr[c], k_ki, scale=-1.0, bias=lc[c]) for c in range(4)]
+        wj = [act(T.wj[:, cc[c]], T.ab[:, cc[c]], RELU, ab[c], k_con, scale=T.nj[:, c:c + 1], bias=T.jn[:, c:c + 1])
+              for c in range(4)]
+        t2 = turn(T.wvt[:, o:o + 128], T.wv[:, o:o + 128], wv)
+        vc = red(T.vc[:, b:b + 1], T.wvt[:, o:o + 128], A.add, t2)
+        v32 = slice(32 * b, 32 * b + 32)
+        bv = ts(T.bv[:, v32], T.z32[:], T.vc[:, b:b + 1], A.add, vc)
+        t3 = turn(T.vt[:, v32], T.bv[:, v32], bv)
+        tj = turn(T.wjt[:, o:o + 128], T.wj[:, o:o + 128], wj)
+
+        cp = []
+        for i, (to, fr, slot, half) in enumerate(moves):
+            k = 96 * b + 48 * half + 16 * slot
+            dst, src = T.gg[to, k:k + 16], T.vt[fr, 32 * b:32 * b + 16]
+            cp.append(vcopy(dst, src, t3, k_gg) if i % 2 == 0 else act(dst, src, COPY, t3, k_gg))
+        jcol = act(T.jj[:, o:o + 128], T.wjt[:, o:o + 128], IDENT, tj, bias=T.rc[:, 2:3], accum_out=T.jcol[:, b:b + 1])
+        g0 = 96 * b
+        f1 = ts(T.c2[:, g0:g0 + 48], T.gg[:, g0:g0 + 48], T.vc[:, b:b + 1], A.is_ge, cp)
+        f2 = ts(T.c2[:, g0 + 48:g0 + 96], T.gg[:, g0 + 48:g0 + 96], T.vc[:, b:b + 1], A.is_gt)
+        n2 = red(T.n2[:, b:b + 1], T.c2[:, g0:g0 + 96], A.add, f1, f2)
+        w2 = ts(T.w2[:, v32], T.kim[:], T.n2[:, b:b + 1], A.is_equal, n2, jcol, s2=T.jcol[:, b:b + 1], op1=A.mult)
+        x0 = 80 * b
+        t4 = turn(T.w2x[:, x0:x0 + 32], T.w2[:, v32], w2)
+        cp = []
+        for i, (to, fr, slot, half) in enumerate(moves):
+            k = x0 + 32 + 16 * slot
+            dst, src = T.w2x[to, k:k + 16], T.w2x[fr, x0:x0 + 16]
+            cp.append(vcopy(dst, src, t4) if i % 2 == 0 or i == 9 else act(dst, src, COPY, t4))
+        lf = red(T.lf[:, b:b + 1], T.w2x[:, x0:x0 + 80], A.add, cp, t4)
+        of = T["of%d" % b]
+        mq, ms = T["mq%d" % b], T["ms%d" % b]
+        oo = vcopy(of[:, 0:1], T.lf[:, b:b + 1], lf)
+        mine = slice(16 * rank, 16 * rank + 16)
+        both = slice(16 * pair[0], 16 * pair[0] + 32)
+        pk = vcopy(mq[:, mine].bitcast(dt.uint32), T.xq[:].bitcast(dt.uint32).indirect(of[:, 0:1]), oo, qx)
+        pz = act(ms[:, mine], T.xs[:].indirect(of[:, 0:1]), COPY, oo, qx)
+
+        far = "far%d" % b
+        arr_q, arr_z = ("nq%d" % b, len(near_eng)), ("nz%d" % b, len(near_eng))
+        wait("g", [pk])
+        send(mq[:, mine].bitcast(dt.uint8), (mate, near_eng, arr_q[0]), (ahead, far_eng, far))
+        wait("g", [pz])
+        send(ms[:, mine], (mate, near_eng, arr_z[0]), (ahead, far_eng, far))
+        wait("g", [arr_q])
+        send(mq[:, both].bitcast(dt.uint8), (rest, far_eng, far))
+        wait("g", [arr_z])
+        send(ms[:, both], (rest, far_eng, far))
+        arrived = [arr_q, arr_z, (far, n_far)]
+
+        if b == 0:
+            p1 = vcopy(T.pq[:].bitcast(dt.uint32), T.xq[:].bitcast(dt.uint32).indirect(T.po[:]), k_po)
+            p2 = act(T.pz[:], T.xs[:].indirect(T.po[:]), COPY, k_po, qx)
+            perm = [p1, p2]
+        if b < R - 1:
+            i1 = ts(T.ind[:, v32], T.rb[:], T.n2[:, b:b + 1], A.add, s2=16.0, op1=A.is_lt)
+            i2 = turn(T.indt[:, v32], T.ind[:, v32], i1)
+            i3 = red(T.tt[:, b:b + 1], T.indt[:, v32], A.add, i2)
+            b4 = slice(4 * b, 4 * b + 4)
+            i4 = ts(T.pen[:, b4], T.lr[:, b4], T.tt[:, b:b + 1], A.is_lt, i3, s2=-BIG, op1=A.mult)
+            sm = tt(T.sm[:, b4], T.B[:, o:o + 128:32], T.pen[:, b4], A.add, i4)
+        if b == 0:
+            qw = quant(T.wq[:], T.ws[:], T.wt[:], lw)
+        l1 = ts(T.lb[:, v32], T.z32[:], T.lf[:, b:b + 1], A.add)
+        l2 = turn(T.lt[:, v32], T.lb[:, v32], l1)
+        load("s", T.ch[b:b + 1, :], T.lt[0:1, 32 * b:32 * b + 16], "dch%d" % b, l2)
+        if b == 0:
+            sc = vcopy(T.sc[:, 0:4], T.B[:, 0:128:32])
+        else:
+            p4, b4 = slice(4 * b - 4, 4 * b), slice(4 * b, 4 * b + 4)
+            m1 = ts(T.m25[:, p4], T.mm[:, p4], -0.25, A.mult)
+            sc = tt(T.sc[:, b4], T.sc[:, p4], T.m25[:, p4], A.add, m1, sc)
+        if b == R - 1:
+            e = [ts(T.sb[:, 32 * c:32 * c + 32], T.z32[:], T.sc[:, 4 * b + c:4 * b + c + 1], A.add, sc) for c in range(4)]
+            e = turn(T.sr[:], T.sb[:], e)
+            for a in range(4):
+                load("s", T.se[0:1, 128 * a:128 * a + 128], T.sr[32 * a:32 * a + 1, :], "dse", e)
+        for f in y_todo:
+            f()
+        y_todo = []
+
+        ready = arrived + [pk, pz]
+        if b < R - 1:
+            tm = []
+            for c in range(4):
+                k = slice(128 * c, 128 * c + 128)
+                tm.append(mm(T.ps[:, 512 * c:512 * c + 128], T.pq[:, k], T.pz[:, k], mq[:], ms[:], *ready, *perm, *bank_free))
+            n = 128 * (b + 1)
+            rd, tb = [None] * 4, [None] * 4
+            for c in range(4):
+                i = 4 * b + c
+                rd[c] = red(T.mm[:, i:i + 1], T.ps[:, 512 * c:512 * c + 128], A.max, tm[c])
+                out, m1, s1 = T.B[:, n + 32 * c:n + 32 * c + 32], T.mm[:, i:i + 1], T.sm[:, i:i + 1]
+                if c < 3:
+                    tb[c] = act(out, T.nq[:], IDENT, rd[c], sm, k_nq, scale=m1, bias=s1)
+                else:
+                    tb[c] = ts(out, T.nq[:], m1, A.mult, rd[c], sm, s2=s1, op1=A.add)
+            bank_free = list(rd)
+        ty = mm(T.py[:, 512 * b:512 * b + 128], T.wq[:], T.ws[:], mq[:], ms[:], *ready, qw)
+
+        def put(b=b, ty=ty):
+            k = slice(128 * b, 128 * b + 128)
+            t = act(T.yo[:, k], T.py[:, 512 * b:512 * b + 128], COPY, ty)
+            load("s", T.y[:, k], T.yo[:, k], "dy%d" % b, t)
+        y_todo.append(put)
+    for f in y_todo:
+        f()
+
+    last = [("loc", R * (2 * len(near_eng) + 4 * len(far_eng))), ("dse", 64)] + [("s" + q, count[q]) for q in count]
+    last += [("dy%d" % b, 16) for b in range(R)] + [("dch%d" % b, 16) for b in range(R)]
+    wait("g", last)

@@ -6,6 +6,7 @@ COPY = ActivationFunctionType.Copy
 IDENT = ActivationFunctionType.Identity
 ABS = ActivationFunctionType.Abs
 RELU = ActivationFunctionType.Relu
+SIGN = ActivationFunctionType.Sign
 A = AluOpType
 BIG = 1e29
 
@@ -20,34 +21,33 @@ SCRATCH = {
     "xq": sb(512, F8), "xs": sb(512, U8),
     "pq": sb(512, F8), "pz": sb(512, U8),
     "uq": sb(128, F8), "us": sb(128, U8), "vq": sb(128, F8), "vs": sb(128, U8), "wq": sb(128, F8), "ws": sb(128, U8),
+    "mq": sb(64 + 128 * R, F8), "ms": sb(64 + 128 * R, U8),
     "ip": sb(1, "int32"), "ir": sb(2, "int32"),
     "rc": sb(4),
     "ki": sb(32),
     "k16": sb(32),
-    "kim": sb(32),
-    "mbig": sb(32),
-    "rb": sb(32),
+    "tp": sb(32), "tau": sb(64, BF),
+    "th": sb(2),
     "c4": sb(4), "jn": sb(4), "nj": sb(4),
     "pm": sb(32), "po": sb(32, "uint16"),
     "zo": sb(8, "uint16"),
-    "nq": sb(32), "z32": sb(32),
+    "nq": sb(32), "z32": sb(32), "low": sb(64),
     "B": sb(128 * R),
     "Q": sb(128 * R),
-    "bm": sb(128 * R), "cmp": sb(640 * R, BF), "junk": sb(640 * R, BF), "jj": sb(128 * R), "lr": sb(4 * R),
-    "ab": sb(128 * R), "wv": sb(128 * R), "wj": sb(128 * R, BF), "wvt": sb(128 * R), "wjt": sb(128 * R, BF), "vc": sb(R),
-    "jcol": sb(R), "bv": sb(32 * R), "vt": sb(32 * R), "gg": sb(96 * R), "c2": sb(96 * R), "n2": sb(R), "w2": sb(32 * R),
-    "w2x": sb(80 * R), "lf": sb(R), "lb": sb(32 * R), "lt": sb(32 * R), "ind": sb(32 * R), "indt": sb(32 * R), "tt": sb(R),
-    "pen": sb(4 * R), "sm": sb(4 * R), "mm": sb(4 * R), "m25": sb(4 * R), "sc": sb(4 * R), "sb": sb(128), "sr": sb(128),
-    "yo": sb(512), "ps": ("psum", [128, 2048], "float32"), "py": ("psum", [128, 2048], "float32"),
+    "ns": sb(R), "cmp": sb(512 * R, BF), "junk": sb(256 * R, BF), "jj": sb(128 * R), "lr": sb(2 * R), "ls": sb(128 * R),
+    "ab": sb(128 * R), "wv": sb(128 * R), "wj": sb(128 * R, BF), "wvt": sb(192 * R), "wjt": sb(128 * R, BF),
+    "bs": sb(96 * R), "jcol": sb(R), "vt": sb(32 * R), "c2": sb(48 * R, BF), "n2": sb(32 * R), "w2": sb(32 * R),
+    "w2t": sb(32 * R), "hh": sb(32 * R), "lb": sb(32 * R), "lt": sb(32 * R), "ind": sb(32 * R), "indt": sb(32 * R),
+    "tt": sb(R), "pen": sb(4 * R), "sm": sb(4 * R), "me": sb(4 * R), "mx": sb(256 * R), "m25": sb(4 * R), "sc": sb(4 * R),
+    "sb": sb(128), "sr": sb(128),
+    "yo": sb(512), "ps": ("psum", [128, 2048], "float32"), "pe": ("psum", [128, 2048], "float32"),
 }
 for _b in range(R):
     SCRATCH["of%d" % _b] = sb(2, "uint16")
-    SCRATCH["mq%d" % _b] = sb(128, F8)
-    SCRATCH["ms%d" % _b] = sb(128, U8)
 
-SEMAPHORES = ["sv", "sa", "st", "sg", "du", "dw", "dse", "loc"]
+SEMAPHORES = ["sv", "sa", "st", "sg", "du", "dw", "dse", "dpad", "loc"]
 SEMAPHORES += ["dx%d" % i for i in range(4)]
-SEMAPHORES += ["%s%d" % (n, b) for n in ("nq", "nz", "far", "dy", "dch") for b in range(R)]
+SEMAPHORES += ["%s%d" % (n, b) for n in ("nq", "nz", "fe", "fl", "dy", "dch") for b in range(R)]
 
 
 def mask_of(engines):
@@ -63,26 +63,37 @@ def rank_program(g, core, T, topo):
     for c in cores:
         if topo.chip(c) not in chips:
             chips.append(topo.chip(c))
+    nch = len(chips)
     on = lambda ch: [r for r in range(len(cores)) if topo.chip(cores[r]) == ch]
-    at = chips.index(topo.chip(core))
+    place = lambda r: chips.index(topo.chip(cores[r]))
+    at = place(rank)
     pair = on(chips[at])
+    me = pair.index(rank)
     mate = [r for r in pair if r != rank]
-    ahead = on(chips[(at + 1) % len(chips)])
-    rest = [on(chips[(at + k) % len(chips)])[pair.index(rank)] for k in (3, 2)]
+    ahead = on(chips[(at + 1) % nch])
+    rest = [on(chips[(at + k) % nch])[me] for k in (3, 2)]
     far_eng = topo.engines(core, cores[ahead[0]])
     near_eng = [e for e in topo.engines(core, cores[mate[0]]) if e not in far_eng]
-    n_far = len(far_eng) * 2 * (len(ahead) + len(rest))
+    n_early, n_late = len(far_eng) * 2 * len(ahead), len(far_eng) * 2 * len(rest)
+
+    def col0(b, r):
+        slot = at if b == R - 1 else (at - place(r) + 1) % nch
+        return 64 + 128 * b + 32 * slot
 
     Q = {"v": g.vector, "a": g.scalar, "t": g.tensor, "g": g, "s": g.sync}
     count = {"v": 0, "a": 0, "t": 0, "g": 0}
     seen = {k: {} for k in Q}
 
-    def wait(q, deps):
-        need = {}
+    def flat(deps, need):
         for d in deps:
-            for s, n in (d if isinstance(d, list) else [d]):
-                need[s] = max(need.get(s, 0), n)
-        for s, n in need.items():
+            if isinstance(d, list):
+                flat(d, need)
+            elif d is not None:
+                need[d[0]] = max(need.get(d[0], 0), d[1])
+        return need
+
+    def wait(q, deps):
+        for s, n in flat(deps, {}).items():
             if seen[q].get(s, 0) < n:
                 Q[q].wait_ge(T.sem[s], n)
                 seen[q][s] = n
@@ -105,6 +116,10 @@ def rank_program(g, core, T, topo):
     def red(out, in_, op, *deps):
         wait("v", deps)
         return done("v", g.vector.tensor_reduce(out, in_, AxisListType.X, op))
+
+    def scan(out, d0, d1, first, op, *deps):
+        wait("v", deps)
+        return done("v", g.vector.tensor_tensor_scan(out, d0, d1, first, op, op))
 
     def turn(out, in_, *deps):
         wait("v", deps)
@@ -134,11 +149,14 @@ def rank_program(g, core, T, topo):
         Q[q].dma_start(out, in_).then_inc(T.sem[sem], 16)
         return (sem, 16)
 
-    def send(view, *groups):
+    def send(view, b, off, n, *groups):
+        cut = lambda r: view(col0(b, r) + off, col0(b, r) + off + n)
         g.remote_dma_fused([
             RemoteDMATransfer(dst_ids=[DstId(rid=topo.addr(cores[r])[0], pnc=topo.addr(cores[r])[1]) for r in to],
-                              dma_engine_mask=mask_of(eng), remote_sem=T.sem[arr], srcs=[view], dsts=[view for r in to])
+                              dma_engine_mask=mask_of(eng), remote_sem=T.sem[arr], srcs=[cut(rank)], dsts=[cut(r) for r in to])
             for to, eng, arr in groups], local_sem=T.sem.loc)
+    codes = lambda i, j: T.mq[:, i:j].bitcast(dt.uint8)
+    plane = lambda i, j: T.ms[:, i:j]
 
     lu = load("a", T.ut[:, 0:64], T.u[:, 0:64], "du")
     lx = [load("s" if i % 2 == 0 else "a", T.xt[:, 512 * i:512 * i + 512], T.x[:, 512 * i:512 * i + 512], "dx%d" % i)
@@ -156,18 +174,22 @@ def rank_program(g, core, T, topo):
     k_pm = iota(T.pm[:], [[32, 4], [128, 4], [16, 2]], 0, **flag)
     k_nq = fill(T.nq[:], -0.25)
     k_z = fill(T.z32[:], 0.0)
-    k_gg = fill(T.gg[:], -BIG)
+    fill(T.low[:], -BIG)
+    fill(T.th[0:64, :], -0.5)
+    fill(T.th[64:128, :], 0.5)
+    for b in range(R):
+        fill(T.wvt[:, 192 * b + 128:192 * b + 192], 0.0)
     a1 = ts(T.ir[:, 0:1], T.ip[:], 31, A.bitwise_and, k_ip)
     a2 = ts(T.ir[:, 1:2], T.ip[:], 15, A.bitwise_and)
     a3 = vcopy(T.rc[:, 3:4], T.ip[:])
     k_rc = vcopy(T.rc[:, 0:2], T.ir[:], a1, a2)
     ts(T.rc[:, 2:3], T.rc[:, 3:4], T.rc[:, 0:1], A.subtract, k_rc, a3, s2=1.0 / 32, op1=A.mult)
-    ts(T.kim[:], T.k16[:], T.rc[:, 0:1], A.subtract, k_16)
-    k_mb = ts(T.mbig[:], T.ki[:], T.rc[:, 0:1], A.is_ge, k_ki, s2=BIG, op1=A.mult)
-    ts(T.rb[:], T.z32[:], T.rc[:, 0:1], A.add, k_z)
+    k_tp = ts(T.tp[:], T.ki[:], T.rc[:, 0:1], A.is_ge, k_ki, s2=0.5, op1=A.subtract)
     k_po = ts(T.po[:], T.pm[:], T.rc[:, 1:2], A.add, k_pm)
     k_jn = ts(T.jn[:], T.c4[:], T.rc[:, 0:1], A.add, k_c4)
-    k_con = ts(T.nj[:], T.jn[:], -1.0, A.mult, k_jn)
+    vcopy(T.tau[:, 0:32], T.tp[:], k_tp)
+    ts(T.tau[:, 32:64], T.tp[:], -1.0, A.mult)
+    k_con = ts(T.nj[:], T.jn[:], -1.0, A.mult, k_jn, k_16)
 
     qu = quant(T.uq[:], T.us[:], T.ut[:], lu, k_u)
     u1 = vcopy(T.vq[:].bitcast(dt.uint32), T.uq[:].bitcast(dt.uint32).indirect(T.zo[:, 0:8]), qu, k_zo)
@@ -185,144 +207,160 @@ def rank_program(g, core, T, topo):
         else:
             tq.append(act(T.Q[h, 0:128], T.ps[h, 512 * i:512 * i + 128], COPY, t))
     tb = [turn(T.B[:, 0:128], T.Q[:, 0:128], *tq, k_con)] * 4
+    load("s", T.mq[:, 0:64].bitcast(dt.uint8), T.xq[:, 0:64].bitcast(dt.uint8), "dpad", qx[0])
+    load("s", T.ms[:, 0:64], T.xs[:, 0:64], "dpad")
+    pad = ("dpad", 32)
     bank_free = list(tq)
     y_todo = []
-    qw = perm = sc = None
+    y_out = []
+    qw = perm = sc = neg = None
 
-    def span(a, n):
+    def span(a, n=1):
         return slice(32 * a, 32 * a + 32 * n)
-    moves = [(span(0, 2), span(2, 2), 0, 1), (span(2, 2), span(0, 2), 0, 0)]
-    for x, slot in ((1, 1), (3, 2)):
-        for a in range(4):
-            moves.append((span(a, 1), span(a ^ x, 1), slot, 1 if (a ^ x) > a else 0))
 
     for b in range(R):
         o = 128 * b
-        if b > 0:
-            tq = [turn(T.Q[:, o:o + 128], T.B[:, o:o + 128], *tb)]
-        bm = [act(T.bm[:, o + 32 * c:o + 32 * c + 32], T.mbig[:], IDENT, tb[c], k_mb,
-                  bias=T.B[:, o + 32 * c:o + 32 * c + 1]) for c in range(4)]
-        lr = []
-        for c in range(4):
-            s = T.B[:, o + 32 * c:o + 32 * c + 1]
-            w = 640 * b + 160 * c
-            d = []
-            if c > 0:
-                d.append(ts(T.cmp[:, w:w + 32 * c], T.Q[:, o:o + 32 * c], s, A.is_ge, tq, tb))
-            d.append(ts(T.cmp[:, w + 32 * c:w + 128], T.Q[:, o + 32 * c:o + 128], s, A.is_gt, tq, tb))
-            d.append(tt(T.cmp[:, w + 128:w + 160], T.Q[:, o + 32 * c:o + 32 * c + 32],
-                        T.bm[:, o + 32 * c:o + 32 * c + 32], A.is_equal, bm[c]))
-            lr.append(act(T.junk[:, w:w + 160], T.cmp[:, w:w + 160], COPY, d, accum_out=T.lr[:, 4 * b + c:4 * b + c + 1]))
         cc = [slice(o + 32 * c, o + 32 * c + 32) for c in range(4)]
-        lc = [T.lr[:, 4 * b + c:4 * b + c + 1] for c in range(4)]
-        wv = [ts(T.wv[:, cc[c]], T.ki[:], lc[c], A.is_equal, lr[c], s2=T.B[:, o + 32 * c:o + 32 * c + 1], op1=A.mult)
-              for c in range(4)]
-        ab = [act(T.ab[:, cc[c]], T.ki[:], ABS, lr[c], k_ki, scale=-1.0, bias=lc[c]) for c in range(4)]
-        wj = [act(T.wj[:, cc[c]], T.ab[:, cc[c]], RELU, ab[c], k_con, scale=T.nj[:, c:c + 1], bias=T.jn[:, c:c + 1])
-              for c in range(4)]
-        t2 = turn(T.wvt[:, o:o + 128], T.wv[:, o:o + 128], wv)
-        vc = red(T.vc[:, b:b + 1], T.wvt[:, o:o + 128], A.add, t2)
-        v32 = slice(32 * b, 32 * b + 32)
-        bv = ts(T.bv[:, v32], T.z32[:], T.vc[:, b:b + 1], A.add, vc)
-        t3 = turn(T.vt[:, v32], T.bv[:, v32], bv)
+        sv = [T.B[:, o + 32 * c:o + 32 * c + 1] for c in range(4)]
+        w = [512 * b + 128 * c for c in range(4)]
+        own = [T.cmp[:, w[c] + 32 * c:w[c] + 32 * c + 32] for c in range(4)]
+        if b == 0:
+            neg = act(T.ns[:, 0:1], sv[0], COPY, tb[0], scale=-1.0)
+        else:
+            tq = [turn(T.Q[:, o:o + 128], T.B[:, o:o + 128], *tb)]
+        sg = [act(T.cmp[:, w[0]:w[0] + 128], T.Q[:, o:o + 128], SIGN, tq, neg, bias=T.ns[:, b:b + 1])]
+        sg += [act(own[c], T.Q[:, cc[c]], SIGN, tq, tb, scale=-1.0, bias=sv[c]) for c in (1, 2, 3)]
+        below = lambda c: ts(T.cmp[:, w[c]:w[c] + 32 * c], T.Q[:, o:o + 32 * c], sv[c], A.is_ge, tq, tb)
+        above = lambda c: ts(T.cmp[:, w[c] + 32 * c + 32:w[c] + 128], T.Q[:, o + 32 * c + 32:o + 128], sv[c], A.is_gt, tq, tb)
+        inside = lambda c: tt(own[c], own[c], T.tau[:, 32:64], A.is_lt, sg[c])
+        d1 = [below(1), above(1)]
+        d0 = tt(own[0], own[0], T.tau[:, 0:32], A.is_gt, sg[0])
+        d1.append(inside(1))
+        d2 = [below(2), above(2), inside(2)]
+        d3 = [below(3), inside(3)]
+        lc = [T.lr[:, 2 * b:2 * b + 1], T.lr[:, 2 * b + 1:2 * b + 2], T.ls[:, o + 63:o + 64], T.ls[:, o + 127:o + 128]]
+        lr = [act(T.junk[:, 256 * b + 128 * c:256 * b + 128 * c + 128], T.cmp[:, w[c]:w[c] + 128], RELU, d, accum_out=lc[c])
+              for c, d in ((0, d0), (1, d1))]
+        lr += [scan(T.ls[:, o + 64 * c - 128:o + 64 * c - 64], T.cmp[:, w[c]:w[c] + 64], T.cmp[:, w[c] + 64:w[c] + 128], 0.0,
+                    A.add, d) for c, d in ((2, d2), (3, d3))]
+        wv = [ts(T.wv[:, cc[c]], T.ki[:], lc[c], A.is_equal, lr[c], s2=sv[c], op1=A.mult) for c in range(4)]
+        wj = []
+        for h in (0, 2):
+            ab = [act(T.ab[:, cc[c]], T.ki[:], ABS, lr[c], k_ki, scale=-1.0, bias=lc[c]) for c in (h, h + 1)]
+            wj += [act(T.wj[:, cc[c]], T.ab[:, cc[c]], RELU, ab[c - h], k_con, scale=T.nj[:, c:c + 1], bias=T.jn[:, c:c + 1])
+                   for c in (h, h + 1)]
+        x0, y0 = 192 * b, 96 * b
+        t2 = turn(T.wvt[:, x0:x0 + 128], T.wv[:, o:o + 128], wv)
+        bs = scan(T.bs[:, y0:y0 + 96], T.wvt[:, x0:x0 + 192:2], T.wvt[:, x0 + 1:x0 + 192:2], 0.0, A.add, t2)
         tj = turn(T.wjt[:, o:o + 128], T.wj[:, o:o + 128], wj)
+        v32 = slice(32 * b, 32 * b + 32)
+        t3 = turn(T.vt[:, v32], T.bs[:, y0 + 64:y0 + 96], bs)
 
-        cp = []
-        for i, (to, fr, slot, half) in enumerate(moves):
-            k = 96 * b + 48 * half + 16 * slot
-            dst, src = T.gg[to, k:k + 16], T.vt[fr, 32 * b:32 * b + 16]
-            cp.append(vcopy(dst, src, t3, k_gg) if i % 2 == 0 else act(dst, src, COPY, t3, k_gg))
+        z0 = 48 * b
+        row = lambda p: T.vt[p, 32 * b:32 * b + 16]
+        vc = lambda p: T.bs[p, y0 + 95:y0 + 96]
+        s3 = [act(T.c2[span(a), z0 + 32:z0 + 48], row(span(a ^ 3)), SIGN, t3, scale=-1.0, bias=vc(span(a))) for a in range(4)]
         jcol = act(T.jj[:, o:o + 128], T.wjt[:, o:o + 128], IDENT, tj, bias=T.rc[:, 2:3], accum_out=T.jcol[:, b:b + 1])
-        g0 = 96 * b
-        f1 = ts(T.c2[:, g0:g0 + 48], T.gg[:, g0:g0 + 48], T.vc[:, b:b + 1], A.is_ge, cp)
-        f2 = ts(T.c2[:, g0 + 48:g0 + 96], T.gg[:, g0 + 48:g0 + 96], T.vc[:, b:b + 1], A.is_gt)
-        n2 = red(T.n2[:, b:b + 1], T.c2[:, g0:g0 + 96], A.add, f1, f2)
-        w2 = ts(T.w2[:, v32], T.kim[:], T.n2[:, b:b + 1], A.is_equal, n2, jcol, s2=T.jcol[:, b:b + 1], op1=A.mult)
-        x0 = 80 * b
-        t4 = turn(T.w2x[:, x0:x0 + 32], T.w2[:, v32], w2)
-        cp = []
-        for i, (to, fr, slot, half) in enumerate(moves):
-            k = x0 + 32 + 16 * slot
-            dst, src = T.w2x[to, k:k + 16], T.w2x[fr, x0:x0 + 16]
-            cp.append(vcopy(dst, src, t4) if i % 2 == 0 or i == 9 else act(dst, src, COPY, t4))
-        lf = red(T.lf[:, b:b + 1], T.w2x[:, x0:x0 + 80], A.add, cp, t4)
+        f = [ts(T.c2[span(0, 2), z0:z0 + 16], row(span(2, 2)), vc(span(0, 2)), A.is_gt, t3),
+             ts(T.c2[span(2, 2), z0:z0 + 16], row(span(0, 2)), vc(span(2, 2)), A.is_ge)]
+        f += [ts(T.c2[span(a), z0 + 16:z0 + 32], row(span(a ^ 1)), vc(span(a)), A.is_ge if a % 2 else A.is_gt)
+              for a in range(4)]
+        f.append(ts(T.c2[:, z0 + 32:z0 + 48], T.c2[:, z0 + 32:z0 + 48], T.th[:, 0:1], A.is_lt, s3))
+        n2 = scan(T.n2[:, 32 * b:32 * b + 24], T.c2[:, z0:z0 + 24], T.c2[:, z0 + 24:z0 + 48], T.rc[:, 0:1], A.add, f)
+        nc = T.n2[:, 32 * b + 23:32 * b + 24]
+        w2 = ts(T.w2[:, v32], T.k16[:], nc, A.is_equal, n2, jcol, s2=T.jcol[:, b:b + 1], op1=A.mult)
+        t4 = turn(T.w2t[:, v32], T.w2[:, v32], w2)
+        hh = scan(T.hh[span(0, 2), v32], T.w2t[span(0, 2), v32], T.w2t[span(2, 2), v32], 0.0, A.add, t4)
+        hc = lambda a: T.hh[span(a), 32 * b + 31:32 * b + 32]
         of = T["of%d" % b]
-        mq, ms = T["mq%d" % b], T["ms%d" % b]
-        oo = vcopy(of[:, 0:1], T.lf[:, b:b + 1], lf)
-        mine = slice(16 * rank, 16 * rank + 16)
-        both = slice(16 * pair[0], 16 * pair[0] + 32)
-        pk = vcopy(mq[:, mine].bitcast(dt.uint32), T.xq[:].bitcast(dt.uint32).indirect(of[:, 0:1]), oo, qx)
-        pz = act(ms[:, mine], T.xs[:].indirect(of[:, 0:1]), COPY, oo, qx)
+        oo = [ts(of[span(a), 0:1], hc(0), hc(1), A.add, hh) for a in range(4)]
+        m0 = col0(b, rank) + 16 * me
+        pk = vcopy(T.mq[:, m0:m0 + 16].bitcast(dt.uint32), T.xq[:].bitcast(dt.uint32).indirect(of[:, 0:1]), oo, qx)
+        pz = act(T.ms[:, m0:m0 + 16], T.xs[:].indirect(of[:, 0:1]), COPY, oo, qx)
 
-        far = "far%d" % b
+        fe, fl = "fe%d" % b, "fl%d" % b
         arr_q, arr_z = ("nq%d" % b, len(near_eng)), ("nz%d" % b, len(near_eng))
         wait("g", [pk])
-        send(mq[:, mine].bitcast(dt.uint8), (mate, near_eng, arr_q[0]), (ahead, far_eng, far))
+        send(codes, b, 16 * me, 16, (mate, near_eng, arr_q[0]), (ahead, far_eng, fe))
         wait("g", [pz])
-        send(ms[:, mine], (mate, near_eng, arr_z[0]), (ahead, far_eng, far))
+        send(plane, b, 16 * me, 16, (mate, near_eng, arr_z[0]), (ahead, far_eng, fe))
         wait("g", [arr_q])
-        send(mq[:, both].bitcast(dt.uint8), (rest, far_eng, far))
+        send(codes, b, 0, 32, (rest, far_eng, fl))
         wait("g", [arr_z])
-        send(ms[:, both], (rest, far_eng, far))
-        arrived = [arr_q, arr_z, (far, n_far)]
+        send(plane, b, 0, 32, (rest, far_eng, fl))
+        early = [arr_q, arr_z, (fe, n_early), pk, pz]
+        ready = early + [(fl, n_late)]
 
         if b == 0:
             p1 = vcopy(T.pq[:].bitcast(dt.uint32), T.xq[:].bitcast(dt.uint32).indirect(T.po[:]), k_po)
             p2 = act(T.pz[:], T.xs[:].indirect(T.po[:]), COPY, k_po, qx)
             perm = [p1, p2]
+        b4 = slice(4 * b, 4 * b + 4)
         if b < R - 1:
-            i1 = ts(T.ind[:, v32], T.rb[:], T.n2[:, b:b + 1], A.add, s2=16.0, op1=A.is_lt)
+            i1 = ts(T.ind[:, v32], T.z32[:], nc, A.add, s2=16.0, op1=A.is_lt)
             i2 = turn(T.indt[:, v32], T.ind[:, v32], i1)
             i3 = red(T.tt[:, b:b + 1], T.indt[:, v32], A.add, i2)
-            b4 = slice(4 * b, 4 * b + 4)
-            i4 = ts(T.pen[:, b4], T.lr[:, b4], T.tt[:, b:b + 1], A.is_lt, i3, s2=-BIG, op1=A.mult)
-            sm = tt(T.sm[:, b4], T.B[:, o:o + 128:32], T.pen[:, b4], A.add, i4)
-        if b == 0:
-            qw = quant(T.wq[:], T.ws[:], T.wt[:], lw)
-        l1 = ts(T.lb[:, v32], T.z32[:], T.lf[:, b:b + 1], A.add)
-        l2 = turn(T.lt[:, v32], T.lb[:, v32], l1)
+            i4 = ts(T.pen[:, 4 * b:4 * b + 2], T.lr[:, 2 * b:2 * b + 2], T.tt[:, b:b + 1], A.is_lt, i3, s2=-BIG, op1=A.mult)
+            i5 = ts(T.pen[:, 4 * b + 2:4 * b + 4], T.ls[:, o + 63:o + 128:64], T.tt[:, b:b + 1], A.is_lt, s2=-BIG, op1=A.mult)
+            sm = tt(T.sm[:, b4], T.B[:, o:o + 128:32], T.pen[:, b4], A.add, i4, i5)
+        l1 = ts(T.lb[span(0), v32], T.z32[span(0), :], hc(0), A.add, s2=hc(1), op1=A.add)
+        l2 = turn(T.lt[span(0), v32], T.lb[span(0), v32], l1)
         load("s", T.ch[b:b + 1, :], T.lt[0:1, 32 * b:32 * b + 16], "dch%d" % b, l2)
         if b == 0:
             sc = vcopy(T.sc[:, 0:4], T.B[:, 0:128:32])
         else:
-            p4, b4 = slice(4 * b - 4, 4 * b), slice(4 * b, 4 * b + 4)
-            m1 = ts(T.m25[:, p4], T.mm[:, p4], -0.25, A.mult)
+            p4 = slice(4 * b - 4, 4 * b)
+            m1 = ts(T.m25[:, p4], T.mx[:, 256 * b - 256 + 63:256 * b:64], -0.25, A.mult)
             sc = tt(T.sc[:, b4], T.sc[:, p4], T.m25[:, p4], A.add, m1, sc)
         if b == R - 1:
             e = [ts(T.sb[:, 32 * c:32 * c + 32], T.z32[:], T.sc[:, 4 * b + c:4 * b + c + 1], A.add, sc) for c in range(4)]
             e = turn(T.sr[:], T.sb[:], e)
             for a in range(4):
                 load("s", T.se[0:1, 128 * a:128 * a + 128], T.sr[32 * a:32 * a + 1, :], "dse", e)
-        for f in y_todo:
-            f()
+        for fn in y_todo:
+            y_out = fn()
         y_todo = []
 
-        ready = arrived + [pk, pz]
+        n0 = 64 + 128 * b
+        mq, ms = T.mq[:, n0:n0 + 128], T.ms[:, n0:n0 + 128]
+        re_ = []
         if b < R - 1:
-            tm = []
-            for c in range(4):
-                k = slice(128 * c, 128 * c + 128)
-                tm.append(mm(T.ps[:, 512 * c:512 * c + 128], T.pq[:, k], T.pz[:, k], mq[:], ms[:], *ready, *perm, *bank_free))
+            piece = lambda c: (T.pq[:, 128 * c:128 * c + 128], T.pz[:, 128 * c:128 * c + 128])
+            te = [mm(T.pe[:, 512 * c:512 * c + 128], *piece(c), T.mq[:, n0 - 64:n0 + 64], T.ms[:, n0 - 64:n0 + 64],
+                     early, perm, pad, y_out) for c in range(4)]
+            re_ = [red(T.me[:, 4 * b + c:4 * b + c + 1], T.pe[:, 512 * c + 64:512 * c + 128], A.max, te[c]) for c in range(4)]
+            if b == 0:
+                qw = quant(T.wq[:], T.ws[:], T.wt[:], lw)
+            tm = [mm(T.ps[:, 512 * c:512 * c + 128], *piece(c), mq, ms, ready, bank_free) for c in range(4)]
             n = 128 * (b + 1)
             rd, tb = [None] * 4, [None] * 4
             for c in range(4):
-                i = 4 * b + c
-                rd[c] = red(T.mm[:, i:i + 1], T.ps[:, 512 * c:512 * c + 128], A.max, tm[c])
-                out, m1, s1 = T.B[:, n + 32 * c:n + 32 * c + 32], T.mm[:, i:i + 1], T.sm[:, i:i + 1]
+                i, k = 4 * b + c, 256 * b + 64 * c
+                rd[c] = scan(T.mx[:, k:k + 64], T.ps[:, 512 * c + 64:512 * c + 128], T.low[:], T.me[:, i:i + 1], A.max,
+                             tm[c], re_[c])
+                out, m1, s1 = T.B[:, n + 32 * c:n + 32 * c + 32], T.mx[:, k + 63:k + 64], T.sm[:, i:i + 1]
                 if c < 3:
                     tb[c] = act(out, T.nq[:], IDENT, rd[c], sm, k_nq, scale=m1, bias=s1)
                 else:
                     tb[c] = ts(out, T.nq[:], m1, A.mult, rd[c], sm, s2=s1, op1=A.add)
+            neg = act(T.ns[:, b + 1:b + 2], T.B[:, n:n + 1], COPY, tb[0], scale=-1.0)
             bank_free = list(rd)
-        ty = mm(T.py[:, 512 * b:512 * b + 128], T.wq[:], T.ws[:], mq[:], ms[:], *ready, qw)
+        ty = mm(T.pe[:, 1536:1664], T.wq[:], T.ws[:], mq, ms, ready, qw, re_, y_out)
 
         def put(b=b, ty=ty):
             k = slice(128 * b, 128 * b + 128)
-            t = act(T.yo[:, k], T.py[:, 512 * b:512 * b + 128], COPY, ty)
+            if b == R - 1:
+                t = [vcopy(T.yo[:, k], T.pe[:, 1536:1664], ty)]
+            else:
+                r = 32 * ((at - 1) % nch)
+                t = [act(T.yo[:, 128 * b + r:128 * b + 128], T.pe[:, 1536:1664 - r], COPY, ty)]
+                if r:
+                    t.append(act(T.yo[:, 128 * b:128 * b + r], T.pe[:, 1664 - r:1664], COPY, ty))
             load("s", T.y[:, k], T.yo[:, k], "dy%d" % b, t)
+            return t
         y_todo.append(put)
-    for f in y_todo:
-        f()
+    for fn in y_todo:
+        fn()
 
     last = [("loc", R * (2 * len(near_eng) + 4 * len(far_eng))), ("dse", 64)] + [("s" + q, count[q]) for q in count]
     last += [("dy%d" % b, 16) for b in range(R)] + [("dch%d" % b, 16) for b in range(R)]

@@ -4,7 +4,6 @@ from concourse.mybir import dt, AluOpType, AxisListType, ActivationFunctionType
 R = 4
 COPY = ActivationFunctionType.Copy
 IDENT = ActivationFunctionType.Identity
-ABS = ActivationFunctionType.Abs
 RELU = ActivationFunctionType.Relu
 SIGN = ActivationFunctionType.Sign
 A = AluOpType
@@ -17,29 +16,26 @@ def sb(n, d="float32"):
 
 F8, U8, BF = "float8_e4m3fn_x4", "uint8", "bfloat16"
 SCRATCH = {
-    "xt": sb(2048, BF), "ut": sb(512, BF), "wt": sb(512, BF),
+    "xt": sb(2048, BF), "ut": sb(576, BF), "wt": sb(512, BF),
     "xq": sb(512, F8), "xs": sb(512, U8),
     "pq": sb(512, F8), "pz": sb(512, U8),
-    "uq": sb(128, F8), "us": sb(128, U8), "vq": sb(128, F8), "vs": sb(128, U8), "wq": sb(128, F8), "ws": sb(128, U8),
+    "uq": sb(128, F8), "us": sb(128, U8), "wq": sb(128, F8), "ws": sb(128, U8),
+    "vq": sb(288, F8), "vs": sb(288, U8),
     "mq": sb(64 + 128 * R, F8), "ms": sb(64 + 128 * R, U8),
-    "ip": sb(1, "int32"), "ir": sb(2, "int32"),
+    "jp": sb(4), "jn": sb(4),
     "rc": sb(4),
-    "ki": sb(32),
-    "k16": sb(32),
-    "tp": sb(32), "tau": sb(64, BF),
-    "th": sb(2),
-    "c4": sb(4), "jn": sb(4), "nj": sb(4),
+    "ki": sb(32), "kr": sb(32), "k16": sb(32),
+    "mb": sb(64),
     "pm": sb(32), "po": sb(32, "uint16"),
-    "zo": sb(8, "uint16"),
+    "zo": sb(2, "uint16"),
     "nq": sb(32), "z32": sb(32), "low": sb(64),
     "B": sb(128 * R),
     "Q": sb(128 * R),
-    "ns": sb(R), "cmp": sb(512 * R, BF), "junk": sb(256 * R, BF), "jj": sb(128 * R), "lr": sb(2 * R), "ls": sb(128 * R),
-    "ab": sb(128 * R), "wv": sb(128 * R), "wj": sb(128 * R, BF), "wvt": sb(192 * R), "wjt": sb(128 * R, BF),
-    "bs": sb(96 * R), "jcol": sb(R), "vt": sb(32 * R), "c2": sb(48 * R, BF), "n2": sb(32 * R), "w2": sb(32 * R),
-    "w2t": sb(32 * R), "hh": sb(32 * R), "lb": sb(32 * R), "lt": sb(32 * R), "ind": sb(32 * R), "indt": sb(32 * R),
-    "tt": sb(R), "pen": sb(4 * R), "sm": sb(4 * R), "me": sb(4 * R), "mx": sb(256 * R), "m25": sb(4 * R), "sc": sb(4 * R),
-    "sb": sb(128), "sr": sb(128),
+    "bm": sb(128 * R), "ns": sb(R), "cmp": sb(640 * R, BF), "junk": sb(320 * R, BF), "ls": sb(320 * R), "wv": sb(128 * R),
+    "wj": sb(128 * R, BF), "wvt": sb(192), "wjt": sb(128 * R, BF), "jj": sb(128 * R), "jcol": sb(R), "bs": sb(96 * R),
+    "vt": sb(32 * R), "c2": sb(48 * R, BF), "n2": sb(32 * R), "w2": sb(32 * R), "w2t": sb(32 * R), "hh": sb(32 * R),
+    "lb": sb(32 * R), "lt": sb(32 * R), "ind": sb(32 * R), "indt": sb(32 * R), "tt": sb(R), "pen": sb(4 * R),
+    "sm": sb(4 * R), "me": sb(4 * R), "mx": sb(256 * R), "m25": sb(4 * R), "sc": sb(4 * R), "sb": sb(128), "sr": sb(128),
     "yo": sb(512), "ps": ("psum", [128, 2048], "float32"), "pe": ("psum", [128, 2048], "float32"),
 }
 for _b in range(R):
@@ -140,9 +136,9 @@ def rank_program(g, core, T, topo):
         wait("a", deps)
         return done("a", g.scalar.activation(out, in_, func, **kw))
 
-    def mm(out, lq, ls, rq, rs, *deps):
+    def mm(out, lq, ls, rq, rs, *deps, start=True, stop=True):
         wait("t", deps)
-        return done("t", g.tensor.matmul_mx(out, lq, ls, rq, rs, True, True))
+        return done("t", g.tensor.matmul_mx(out, lq, ls, rq, rs, start, stop))
 
     def load(q, out, in_, sem, *deps):
         wait(q, deps)
@@ -158,122 +154,150 @@ def rank_program(g, core, T, topo):
     codes = lambda i, j: T.mq[:, i:j].bitcast(dt.uint8)
     plane = lambda i, j: T.ms[:, i:j]
 
+    def span(a, n=1):
+        return slice(32 * a, 32 * a + 32 * n)
+
     lu = load("a", T.ut[:, 0:64], T.u[:, 0:64], "du")
     lx = [load("s" if i % 2 == 0 else "a", T.xt[:, 512 * i:512 * i + 512], T.x[:, 512 * i:512 * i + 512], "dx%d" % i)
           for i in range(4)]
     lw = load("s", T.wt[:], T.w[:], "dw", lx[0])
 
-    iota = lambda out, pat, cm, **kw: done("g", g.iota(out, pat, 0, cm, **kw))
-    flag = {"allow_small_or_imprecise_dtypes": True}
+    iota = lambda out, pat, cm, base=0: done("g", g.iota(out, pat, base, cm, allow_small_or_imprecise_dtypes=True))
+    k_u = fill(T.ut[:, 64:576], 0.0)
+    k_rc = [fill(T.rc[span(a), 3:4], 32.0 * a) for a in range(4)]
     k_zo = fill(T.zo[:], 0)
-    k_u = fill(T.ut[:, 64:512], 0.0)
-    k_ip = iota(T.ip[:], [[0, 1]], 1)
-    k_ki = iota(T.ki[:], [[1, 32]], 0, **flag)
-    k_16 = iota(T.k16[:], [[0, 2], [1, 16]], 0, **flag)
-    k_c4 = iota(T.c4[:], [[32, 4]], 0, **flag)
-    k_pm = iota(T.pm[:], [[32, 4], [128, 4], [16, 2]], 0, **flag)
+    k_jp = iota(T.jp[:], [[32, 4]], 1)
+    k_ki = iota(T.ki[:], [[1, 32]], 0)
+    iota(T.k16[:], [[0, 2], [1, 16]], 0)
+    iota(T.kr[:], [[-1, 32]], 0, base=128)
+    k_pm = iota(T.pm[:], [[32, 4], [128, 4], [16, 2]], 0)
+    k_g = iota(T.wvt[:, 128:192], [[0, 64]], 0)
+    qz = [quant(T.vq[:, i:i + 128], T.vs[:, i:i + 128], T.ut[:, 64:576], k_u) for i in (0, 160)]
+    k_jn = ts(T.jn[:], T.jp[:], T.rc[:, 3:4], A.subtract, k_jp, k_rc)
+    ts(T.rc[:, 1:2], T.rc[:, 3:4], 1.0 / 32, A.mult)
+    ts(T.rc[:, 2:3], T.rc[:, 3:4], 64.0, A.is_ge)
     k_nq = fill(T.nq[:], -0.25)
-    k_z = fill(T.z32[:], 0.0)
+    fill(T.z32[:], 0.0)
     fill(T.low[:], -BIG)
-    fill(T.th[0:64, :], -0.5)
-    fill(T.th[64:128, :], 0.5)
-    for b in range(R):
-        fill(T.wvt[:, 192 * b + 128:192 * b + 192], 0.0)
-    a1 = ts(T.ir[:, 0:1], T.ip[:], 31, A.bitwise_and, k_ip)
-    a2 = ts(T.ir[:, 1:2], T.ip[:], 15, A.bitwise_and)
-    a3 = vcopy(T.rc[:, 3:4], T.ip[:])
-    k_rc = vcopy(T.rc[:, 0:2], T.ir[:], a1, a2)
-    ts(T.rc[:, 2:3], T.rc[:, 3:4], T.rc[:, 0:1], A.subtract, k_rc, a3, s2=1.0 / 32, op1=A.mult)
-    k_tp = ts(T.tp[:], T.ki[:], T.rc[:, 0:1], A.is_ge, k_ki, s2=0.5, op1=A.subtract)
-    k_po = ts(T.po[:], T.pm[:], T.rc[:, 1:2], A.add, k_pm)
-    k_jn = ts(T.jn[:], T.c4[:], T.rc[:, 0:1], A.add, k_c4)
-    vcopy(T.tau[:, 0:32], T.tp[:], k_tp)
-    ts(T.tau[:, 32:64], T.tp[:], -1.0, A.mult)
-    k_con = ts(T.nj[:], T.jn[:], -1.0, A.mult, k_jn, k_16)
 
-    qu = quant(T.uq[:], T.us[:], T.ut[:], lu, k_u)
-    u1 = vcopy(T.vq[:].bitcast(dt.uint32), T.uq[:].bitcast(dt.uint32).indirect(T.zo[:, 0:8]), qu, k_zo)
-    u2 = act(T.vs[:], T.us[:].indirect(T.zo[:, 0:8]), COPY, qu, k_zo)
-    tq, qx = [], []
+    qu = quant(T.uq[:], T.us[:], T.ut[:, 0:512], lu, k_u)
+    q32 = T.jn[:, 0:1]
+    ts(T.mb[:, 0:32], T.ki[:], q32, A.is_ge, k_ki, k_jn, s2=BIG, op1=A.mult)
+    ts(T.mb[:, 32:64], T.ki[:], q32, A.is_lt, s2=BIG, op1=A.mult)
+    k_con = ts(T.rc[:, 0:1], q32, 16.0, A.is_ge, s2=-16.0, op1=A.mult)
+    u1 = vcopy(T.vq[:, 128:160].bitcast(dt.uint32), T.uq[:].bitcast(dt.uint32).indirect(T.zo[:, 0:2]), qu, k_zo)
+    u2 = act(T.vs[:, 128:160], T.us[:].indirect(T.zo[:, 0:2]), COPY, qu, k_zo)
+    qx = []
     for i in range(4):
         c = slice(128 * i, 128 * i + 128)
         qx.append(quant(T.xq[:, c], T.xs[:, c], T.xt[:, 512 * i:512 * i + 512], lx[i]))
+    first = [None, None]
     for i in range(4):
-        c = slice(128 * i, 128 * i + 128)
-        h = slice(32 * i, 32 * i + 32)
-        t = mm(T.ps[:, 512 * i:512 * i + 128], T.vq[:], T.vs[:], T.xq[:, c], T.xs[:, c], u1, u2, qx[i])
-        if i % 2 == 0:
-            tq.append(vcopy(T.Q[h, 0:128], T.ps[h, 512 * i:512 * i + 128], t))
-        else:
-            tq.append(act(T.Q[h, 0:128], T.ps[h, 512 * i:512 * i + 128], COPY, t))
-    tb = [turn(T.B[:, 0:128], T.Q[:, 0:128], *tq, k_con)] * 4
+        c, h = slice(128 * i, 128 * i + 128), slice(128 - 32 * i, 256 - 32 * i)
+        for k in range(2):
+            first[k] = mm(T.ps[:, 512 * k:512 * k + 128], T.vq[:, h], T.vs[:, h], T.xq[:, c], T.xs[:, c], u1, u2, qz, qx[i],
+                          start=i == 0, stop=i == 3)
+    tb = [turn(T.B[:, 0:128], T.ps[:, 0:128], first[0], k_con)] * 4
+    tq = first[1]
+    k_po = ts(T.po[:], T.pm[:], q32, A.add, k_pm, s2=T.rc[:, 0:1], op1=A.add)
     load("s", T.mq[:, 0:64].bitcast(dt.uint8), T.xq[:, 0:64].bitcast(dt.uint8), "dpad", qx[0])
     load("s", T.ms[:, 0:64], T.xs[:, 0:64], "dpad")
     pad = ("dpad", 32)
-    bank_free = list(tq)
     y_todo = []
     y_out = []
-    qw = perm = sc = neg = None
+    qw = perm = sc = neg = tie = bank_free = None
 
-    def span(a, n=1):
-        return slice(32 * a, 32 * a + 32 * n)
+    def mask(b, c):
+        k = 128 * b + 32 * c
+        return act(T.bm[:, k:k + 32], T.mb[:, 32:64] if c == 3 else T.mb[:, 0:32], IDENT, tb[c], k_con, bias=T.B[:, k:k + 1])
 
     for b in range(R):
         o = 128 * b
-        cc = [slice(o + 32 * c, o + 32 * c + 32) for c in range(4)]
+        more = b < R - 1
         sv = [T.B[:, o + 32 * c:o + 32 * c + 1] for c in range(4)]
-        w = [512 * b + 128 * c for c in range(4)]
-        own = [T.cmp[:, w[c] + 32 * c:w[c] + 32 * c + 32] for c in range(4)]
-        if b == 0:
-            neg = act(T.ns[:, 0:1], sv[0], COPY, tb[0], scale=-1.0)
+        cm = lambda i, n: T.cmp[:, 640 * b + i:640 * b + i + n]
+        qv = lambda i, n: T.Q[:, o + i:o + i + n] if b else T.ps[:, i:i + n]
+        qa = T.Q[:, o:o + 128] if b else T.ps[:, 512:640]
+        bm = lambda c: T.bm[:, o + 32 * c:o + 32 * c + 32]
+        if b > 0:
+            turn(T.Q[:, o:o + 96], T.B[:, o:o + 96], tb[0:3])
+            tq = turn(T.Q[:, o + 96:o + 128], T.B[:, o + 96:o + 128], tb[3])
+            tie[3] = mask(b, 3)
         else:
-            tq = [turn(T.Q[:, o:o + 128], T.B[:, o:o + 128], *tb)]
-        sg = [act(T.cmp[:, w[0]:w[0] + 128], T.Q[:, o:o + 128], SIGN, tq, neg, bias=T.ns[:, b:b + 1])]
-        sg += [act(own[c], T.Q[:, cc[c]], SIGN, tq, tb, scale=-1.0, bias=sv[c]) for c in (1, 2, 3)]
-        below = lambda c: ts(T.cmp[:, w[c]:w[c] + 32 * c], T.Q[:, o:o + 32 * c], sv[c], A.is_ge, tq, tb)
-        above = lambda c: ts(T.cmp[:, w[c] + 32 * c + 32:w[c] + 128], T.Q[:, o + 32 * c + 32:o + 128], sv[c], A.is_gt, tq, tb)
-        inside = lambda c: tt(own[c], own[c], T.tau[:, 32:64], A.is_lt, sg[c])
-        d1 = [below(1), above(1)]
-        d0 = tt(own[0], own[0], T.tau[:, 0:32], A.is_gt, sg[0])
-        d1.append(inside(1))
-        d2 = [below(2), above(2), inside(2)]
-        d3 = [below(3), inside(3)]
-        lc = [T.lr[:, 2 * b:2 * b + 1], T.lr[:, 2 * b + 1:2 * b + 2], T.ls[:, o + 63:o + 64], T.ls[:, o + 127:o + 128]]
-        lr = [act(T.junk[:, 256 * b + 128 * c:256 * b + 128 * c + 128], T.cmp[:, w[c]:w[c] + 128], RELU, d, accum_out=lc[c])
-              for c, d in ((0, d0), (1, d1))]
-        lr += [scan(T.ls[:, o + 64 * c - 128:o + 64 * c - 64], T.cmp[:, w[c]:w[c] + 64], T.cmp[:, w[c] + 64:w[c] + 128], 0.0,
-                    A.add, d) for c, d in ((2, d2), (3, d3))]
-        wv = [ts(T.wv[:, cc[c]], T.ki[:], lc[c], A.is_equal, lr[c], s2=sv[c], op1=A.mult) for c in range(4)]
-        wj = []
-        for h in (0, 2):
-            ab = [act(T.ab[:, cc[c]], T.ki[:], ABS, lr[c], k_ki, scale=-1.0, bias=lc[c]) for c in (h, h + 1)]
-            wj += [act(T.wj[:, cc[c]], T.ab[:, cc[c]], RELU, ab[c - h], k_con, scale=T.nj[:, c:c + 1], bias=T.jn[:, c:c + 1])
-                   for c in (h, h + 1)]
-        x0, y0 = 192 * b, 96 * b
-        t2 = turn(T.wvt[:, x0:x0 + 128], T.wv[:, o:o + 128], wv)
-        bs = scan(T.bs[:, y0:y0 + 96], T.wvt[:, x0:x0 + 192:2], T.wvt[:, x0 + 1:x0 + 192:2], 0.0, A.add, t2)
+            neg = act(T.ns[:, 0:1], sv[0], COPY, tb[0], scale=-1.0)
+            tie = [None] * 4
+            tie[3], tie[0] = mask(b, 3), mask(b, 0)
+            for c in (1, 2):
+                tie[c] = ts(bm(c), T.mb[:, 0:32], sv[c], A.add, tb)
+        s3 = act(cm(480, 128), qa, SIGN, tq, tb, scale=-1.0, bias=sv[3])
+        s0 = act(cm(0, 128), qa, SIGN, neg, bias=T.ns[:, b:b + 1])
+        tv = tq if b else tb
+        eq = lambda c: tt(cm(160 * c + 128, 32), qv(32 * c, 32), bm(c), A.is_equal, tv, tie[c])
+        cmpv = lambda c: [ts(cm(160 * c, 32 * c), qv(0, 32 * c), sv[c], A.is_ge, tv, tb),
+                          ts(cm(160 * c + 32 * c, 128 - 32 * c), qv(32 * c, 128 - 32 * c), sv[c], A.is_gt)]
+        if b > 0:
+            e0, e3 = eq(0), eq(3)
+            d1 = cmpv(1) + [eq(1)]
+            d2 = cmpv(2) + [eq(2)]
+        else:
+            d1, d2 = cmpv(1), cmpv(2)
+            e3, e0 = eq(3), eq(0)
+            d1.append(eq(1))
+            d2.append(eq(2))
+            bank_free = [d1, d2, s0]
+        l0 = 320 * b
+        lc = [T.ls[:, l0 + k:l0 + k + 1] for k in (79, 159, 239, 318)]
+        kk = [T.ki[:]] * 3 + [T.kr[:]]
+        lr = [None] * 4
+        for c, d, k in ((3, [s3, e3], 160), (0, [s0, e0], 0)):
+            lr[c] = act(T.junk[:, l0 + k:l0 + k + 160], cm(160 * c, 160), RELU, d, accum_out=lc[c])
+        for c, d in ((1, d1), (2, d2)):
+            lr[c] = scan(T.ls[:, l0 + 80 * c:l0 + 80 * c + 80], cm(160 * c, 80), cm(160 * c + 80, 80), 0.0, A.add, d)
+        cc = [slice(o + 32 * c, o + 32 * c + 32) for c in range(4)]
+        wv = [ts(T.wv[:, cc[c]], kk[c], lc[c], A.is_equal, lr[c], k_g, s2=sv[c], op1=A.mult)
+              for c in ((3, 1, 0, 2) if b else (3, 1, 2, 0))]
+        wj = [ts(T.wj[:, cc[c]], kk[c], lc[c], A.is_equal, s2=T.jn[:, c:c + 1], op1=A.mult) for c in range(4)]
+        y0, z0, v32, b4 = 96 * b, 48 * b, slice(32 * b, 32 * b + 32), slice(4 * b, 4 * b + 4)
+        t2 = turn(T.wvt[:, 0:128], T.wv[:, o:o + 128], wv)
         tj = turn(T.wjt[:, o:o + 128], T.wj[:, o:o + 128], wj)
-        v32 = slice(32 * b, 32 * b + 32)
+        jcol = act(T.jj[:, o:o + 128], T.wjt[:, o:o + 128], IDENT, tj, bias=T.rc[:, 1:2], accum_out=T.jcol[:, b:b + 1])
+        if more:
+            r3 = ts(T.ls[:, l0 + 319:l0 + 320], lc[3], -1.0, A.mult, s2=128.0, op1=A.add)
+        bs = scan(T.bs[:, y0:y0 + 96], T.wvt[:, 0:192:2], T.wvt[:, 1:192:2], 0.0, A.add, t2)
+        if b == 0:
+            sc = vcopy(T.sc[:, 0:4], T.B[:, 0:128:32])
+        else:
+            m1 = ts(T.m25[:, 4 * b - 4:4 * b], T.mx[:, 256 * b - 256 + 63:256 * b:64], -0.25, A.mult)
         t3 = turn(T.vt[:, v32], T.bs[:, y0 + 64:y0 + 96], bs)
 
-        z0 = 48 * b
         row = lambda p: T.vt[p, 32 * b:32 * b + 16]
         vc = lambda p: T.bs[p, y0 + 95:y0 + 96]
-        s3 = [act(T.c2[span(a), z0 + 32:z0 + 48], row(span(a ^ 3)), SIGN, t3, scale=-1.0, bias=vc(span(a))) for a in range(4)]
-        jcol = act(T.jj[:, o:o + 128], T.wjt[:, o:o + 128], IDENT, tj, bias=T.rc[:, 2:3], accum_out=T.jcol[:, b:b + 1])
-        f = [ts(T.c2[span(0, 2), z0:z0 + 16], row(span(2, 2)), vc(span(0, 2)), A.is_gt, t3),
-             ts(T.c2[span(2, 2), z0:z0 + 16], row(span(0, 2)), vc(span(2, 2)), A.is_ge)]
-        f += [ts(T.c2[span(a), z0 + 16:z0 + 32], row(span(a ^ 1)), vc(span(a)), A.is_ge if a % 2 else A.is_gt)
-              for a in range(4)]
-        f.append(ts(T.c2[:, z0 + 32:z0 + 48], T.c2[:, z0 + 32:z0 + 48], T.th[:, 0:1], A.is_lt, s3))
-        n2 = scan(T.n2[:, 32 * b:32 * b + 24], T.c2[:, z0:z0 + 24], T.c2[:, z0 + 24:z0 + 48], T.rc[:, 0:1], A.add, f)
-        nc = T.n2[:, 32 * b + 23:32 * b + 24]
+        c2 = lambda p, k: T.c2[p, z0 + 16 * k:z0 + 16 * k + 16]
+        sx = [act(c2(span(a), 2), row(span(a ^ 3)), SIGN, t3, scale=-1.0, bias=vc(span(a))) for a in range(3)]
+        f = [ts(c2(span(0, 2), 0), row(span(2, 2)), vc(span(0, 2)), A.is_gt, t3),
+             ts(c2(span(2, 2), 0), row(span(0, 2)), vc(span(2, 2)), A.is_ge)]
+        f += [ts(c2(span(a), 1), row(span(a ^ 1)), vc(span(a)), A.is_ge if a % 2 else A.is_gt) for a in range(4)]
+        f.append(ts(c2(span(3), 2), row(span(0)), vc(span(3)), A.is_ge))
+        f.append(ts(c2(span(0, 3), 2), c2(span(0, 3), 2), T.rc[span(0, 3), 2:3], A.is_lt, sx))
+        if b > 0:
+            sc = tt(T.sc[:, b4], T.sc[:, 4 * b - 4:4 * b], T.m25[:, 4 * b - 4:4 * b], A.add, m1, sc)
+        n2 = scan(T.n2[:, 32 * b:32 * b + 24], T.c2[:, z0:z0 + 24], T.c2[:, z0 + 24:z0 + 48], q32, A.add, f)
+        nc, tc = T.n2[:, 32 * b + 23:32 * b + 24], T.tt[:, b:b + 1]
         w2 = ts(T.w2[:, v32], T.k16[:], nc, A.is_equal, n2, jcol, s2=T.jcol[:, b:b + 1], op1=A.mult)
+        if more:
+            i1 = ts(T.ind[:, v32], T.z32[:], nc, A.add, s2=16.0, op1=A.is_lt)
         t4 = turn(T.w2t[:, v32], T.w2[:, v32], w2)
+        if more:
+            i2 = turn(T.indt[:, v32], T.ind[:, v32], i1)
         hh = scan(T.hh[span(0, 2), v32], T.w2t[span(0, 2), v32], T.w2t[span(2, 2), v32], 0.0, A.add, t4)
+        if more:
+            i3 = red(tc, T.indt[:, v32], A.add, i2)
         hc = lambda a: T.hh[span(a), 32 * b + 31:32 * b + 32]
         of = T["of%d" % b]
         oo = [ts(of[span(a), 0:1], hc(0), hc(1), A.add, hh) for a in range(4)]
+        l1 = ts(T.lb[span(0), v32], T.z32[span(0), :], hc(0), A.add, s2=hc(1), op1=A.add)
+        if more:
+            i4 = ts(T.pen[:, b4], T.ls[:, l0 + 79:l0 + 320:80], tc, A.is_lt, i3, r3, s2=-BIG, op1=A.mult)
         m0 = col0(b, rank) + 16 * me
         pk = vcopy(T.mq[:, m0:m0 + 16].bitcast(dt.uint32), T.xq[:].bitcast(dt.uint32).indirect(of[:, 0:1]), oo, qx)
         pz = act(T.ms[:, m0:m0 + 16], T.xs[:].indirect(of[:, 0:1]), COPY, oo, qx)
@@ -291,28 +315,16 @@ def rank_program(g, core, T, topo):
         early = [arr_q, arr_z, (fe, n_early), pk, pz]
         ready = early + [(fl, n_late)]
 
+        l2 = turn(T.lt[span(0), v32], T.lb[span(0), v32], l1)
+        load("s", T.ch[b:b + 1, :], T.lt[0:1, 32 * b:32 * b + 16], "dch%d" % b, l2)
+        if more:
+            sm = tt(T.sm[:, b4], T.B[:, o:o + 128:32], T.pen[:, b4], A.add, i4)
         if b == 0:
             p1 = vcopy(T.pq[:].bitcast(dt.uint32), T.xq[:].bitcast(dt.uint32).indirect(T.po[:]), k_po)
             p2 = act(T.pz[:], T.xs[:].indirect(T.po[:]), COPY, k_po, qx)
             perm = [p1, p2]
-        b4 = slice(4 * b, 4 * b + 4)
-        if b < R - 1:
-            i1 = ts(T.ind[:, v32], T.z32[:], nc, A.add, s2=16.0, op1=A.is_lt)
-            i2 = turn(T.indt[:, v32], T.ind[:, v32], i1)
-            i3 = red(T.tt[:, b:b + 1], T.indt[:, v32], A.add, i2)
-            i4 = ts(T.pen[:, 4 * b:4 * b + 2], T.lr[:, 2 * b:2 * b + 2], T.tt[:, b:b + 1], A.is_lt, i3, s2=-BIG, op1=A.mult)
-            i5 = ts(T.pen[:, 4 * b + 2:4 * b + 4], T.ls[:, o + 63:o + 128:64], T.tt[:, b:b + 1], A.is_lt, s2=-BIG, op1=A.mult)
-            sm = tt(T.sm[:, b4], T.B[:, o:o + 128:32], T.pen[:, b4], A.add, i4, i5)
-        l1 = ts(T.lb[span(0), v32], T.z32[span(0), :], hc(0), A.add, s2=hc(1), op1=A.add)
-        l2 = turn(T.lt[span(0), v32], T.lb[span(0), v32], l1)
-        load("s", T.ch[b:b + 1, :], T.lt[0:1, 32 * b:32 * b + 16], "dch%d" % b, l2)
-        if b == 0:
-            sc = vcopy(T.sc[:, 0:4], T.B[:, 0:128:32])
-        else:
-            p4 = slice(4 * b - 4, 4 * b)
-            m1 = ts(T.m25[:, p4], T.mx[:, 256 * b - 256 + 63:256 * b:64], -0.25, A.mult)
-            sc = tt(T.sc[:, b4], T.sc[:, p4], T.m25[:, p4], A.add, m1, sc)
-        if b == R - 1:
+            qw = quant(T.wq[:], T.ws[:], T.wt[:], lw)
+        if not more:
             e = [ts(T.sb[:, 32 * c:32 * c + 32], T.z32[:], T.sc[:, 4 * b + c:4 * b + c + 1], A.add, sc) for c in range(4)]
             e = turn(T.sr[:], T.sb[:], e)
             for a in range(4):
@@ -324,13 +336,11 @@ def rank_program(g, core, T, topo):
         n0 = 64 + 128 * b
         mq, ms = T.mq[:, n0:n0 + 128], T.ms[:, n0:n0 + 128]
         re_ = []
-        if b < R - 1:
+        if more:
             piece = lambda c: (T.pq[:, 128 * c:128 * c + 128], T.pz[:, 128 * c:128 * c + 128])
             te = [mm(T.pe[:, 512 * c:512 * c + 128], *piece(c), T.mq[:, n0 - 64:n0 + 64], T.ms[:, n0 - 64:n0 + 64],
                      early, perm, pad, y_out) for c in range(4)]
             re_ = [red(T.me[:, 4 * b + c:4 * b + c + 1], T.pe[:, 512 * c + 64:512 * c + 128], A.max, te[c]) for c in range(4)]
-            if b == 0:
-                qw = quant(T.wq[:], T.ws[:], T.wt[:], lw)
             tm = [mm(T.ps[:, 512 * c:512 * c + 128], *piece(c), mq, ms, ready, bank_free) for c in range(4)]
             n = 128 * (b + 1)
             rd, tb = [None] * 4, [None] * 4
@@ -344,6 +354,7 @@ def rank_program(g, core, T, topo):
                 else:
                     tb[c] = ts(out, T.nq[:], m1, A.mult, rd[c], sm, s2=s1, op1=A.add)
             neg = act(T.ns[:, b + 1:b + 2], T.B[:, n:n + 1], COPY, tb[0], scale=-1.0)
+            tie = [mask(b + 1, c) for c in range(3)] + [None]
             bank_free = list(rd)
         ty = mm(T.pe[:, 1536:1664], T.wq[:], T.ws[:], mq, ms, ready, qw, re_, y_out)
 

@@ -4,6 +4,7 @@ from concourse.mybir import dt, AluOpType, AxisListType, ActivationFunctionType
 R = 4
 COPY = ActivationFunctionType.Copy
 IDENT = ActivationFunctionType.Identity
+ABS = ActivationFunctionType.Abs
 RELU = ActivationFunctionType.Relu
 SIGN = ActivationFunctionType.Sign
 A = AluOpType
@@ -21,21 +22,21 @@ SCRATCH = {
     "pq": sb(512, F8), "pz": sb(512, U8),
     "uq": sb(128, F8), "us": sb(128, U8), "wq": sb(128, F8), "ws": sb(128, U8),
     "vq": sb(288, F8), "vs": sb(288, U8),
-    "mq": sb(64 + 128 * R, F8), "ms": sb(64 + 128 * R, U8),
-    "jp": sb(4), "jn": sb(4),
+    "mq": sb(96 + 128 * R, F8), "ms": sb(96 + 128 * R, U8),
+    "jp": sb(4), "jn": sb(4), "nj": sb(4),
     "rc": sb(4),
     "ki": sb(32), "kr": sb(32), "k16": sb(32),
     "mb": sb(64),
     "pm": sb(32), "po": sb(32, "uint16"),
     "zo": sb(2, "uint16"),
-    "nq": sb(32), "z32": sb(32), "low": sb(64),
+    "nq": sb(32), "z32": sb(32), "low": sb(96),
     "B": sb(128 * R),
     "Q": sb(128 * R),
     "bm": sb(128 * R), "ns": sb(R), "cmp": sb(640 * R, BF), "junk": sb(320 * R, BF), "ls": sb(320 * R), "wv": sb(128 * R),
-    "wj": sb(128 * R, BF), "wvt": sb(192), "wjt": sb(128 * R, BF), "jj": sb(128 * R), "jcol": sb(R), "bs": sb(96 * R),
-    "vt": sb(32 * R), "c2": sb(48 * R, BF), "n2": sb(32 * R), "w2": sb(32 * R), "w2t": sb(32 * R), "hh": sb(32 * R),
+    "ab": sb(128 * R), "wj": sb(128 * R, BF), "wvt": sb(160), "wjt": sb(128 * R, BF), "jj": sb(128 * R), "jcol": sb(R),
+    "bs": sb(96), "vt": sb(64 * R), "c2": sb(64, BF), "n2": sb(32 * R), "w2": sb(32 * R), "w2t": sb(32 * R), "hh": sb(32 * R),
     "lb": sb(32 * R), "lt": sb(32 * R), "ind": sb(32 * R), "indt": sb(32 * R), "tt": sb(R), "pen": sb(4 * R),
-    "sm": sb(4 * R), "me": sb(4 * R), "mx": sb(256 * R), "m25": sb(4 * R), "sc": sb(4 * R), "sb": sb(128), "sr": sb(128),
+    "sm": sb(4 * R), "me": sb(4 * R), "mx": sb(384 * R), "m25": sb(4 * R), "sc": sb(4 * R), "sb": sb(128), "sr": sb(128),
     "yo": sb(512), "ps": ("psum", [128, 2048], "float32"), "pe": ("psum", [128, 2048], "float32"),
 }
 for _b in range(R):
@@ -43,7 +44,7 @@ for _b in range(R):
 
 SEMAPHORES = ["sv", "sa", "st", "sg", "du", "dw", "dse", "dpad", "loc"]
 SEMAPHORES += ["dx%d" % i for i in range(4)]
-SEMAPHORES += ["%s%d" % (n, b) for n in ("nq", "nz", "fe", "fl", "dy", "dch") for b in range(R)]
+SEMAPHORES += ["%s%d" % (n, b) for n in ("nq", "nz", "fq", "fz", "fw", "dy", "dch") for b in range(R)]
 
 
 def mask_of(engines):
@@ -66,18 +67,16 @@ def rank_program(g, core, T, topo):
     pair = on(chips[at])
     me = pair.index(rank)
     mate = [r for r in pair if r != rank]
-    ahead = on(chips[(at + 1) % nch])
-    rest = [on(chips[(at + k) % nch])[me] for k in (3, 2)]
-    far_eng = topo.engines(core, cores[ahead[0]])
+    cx, cy, cz = [on(chips[(at + k) % nch]) for k in (1, 2, 3)]
+    far_eng = topo.engines(core, cores[cx[0]])
     near_eng = [e for e in topo.engines(core, cores[mate[0]]) if e not in far_eng]
-    n_early, n_late = len(far_eng) * 2 * len(ahead), len(far_eng) * 2 * len(rest)
+    nf, nn = len(far_eng), len(near_eng)
 
-    def col0(b, r):
-        slot = at if b == R - 1 else (at - place(r) + 1) % nch
-        return 64 + 128 * b + 32 * slot
+    def col0(b, r, ch):
+        return 96 + 128 * b + 32 * ((ch - place(r)) % nch)
 
     Q = {"v": g.vector, "a": g.scalar, "t": g.tensor, "g": g, "s": g.sync}
-    count = {"v": 0, "a": 0, "t": 0, "g": 0}
+    count = {"v": 0, "a": 0, "t": 0, "g": 0, "loc": 0}
     seen = {k: {} for k in Q}
 
     def flat(deps, need):
@@ -145,12 +144,14 @@ def rank_program(g, core, T, topo):
         Q[q].dma_start(out, in_).then_inc(T.sem[sem], 16)
         return (sem, 16)
 
-    def send(view, b, off, n, *groups):
-        cut = lambda r: view(col0(b, r) + off, col0(b, r) + off + n)
+    def send(view, b, ch, off, n, *groups):
+        cut = lambda r: view(col0(b, r, ch) + off, col0(b, r, ch) + off + n)
         g.remote_dma_fused([
             RemoteDMATransfer(dst_ids=[DstId(rid=topo.addr(cores[r])[0], pnc=topo.addr(cores[r])[1]) for r in to],
-                              dma_engine_mask=mask_of(eng), remote_sem=T.sem[arr], srcs=[cut(rank)], dsts=[cut(r) for r in to])
+                              dma_engine_mask=mask_of(eng), remote_sem=T.sem["%s%d" % (arr, b)], srcs=[cut(rank)],
+                              dsts=[cut(r) for r in to])
             for to, eng, arr in groups], local_sem=T.sem.loc)
+        count["loc"] += sum(len(eng) for to, eng, arr in groups)
     codes = lambda i, j: T.mq[:, i:j].bitcast(dt.uint8)
     plane = lambda i, j: T.ms[:, i:j]
 
@@ -160,7 +161,7 @@ def rank_program(g, core, T, topo):
     lu = load("a", T.ut[:, 0:64], T.u[:, 0:64], "du")
     lx = [load("s" if i % 2 == 0 else "a", T.xt[:, 512 * i:512 * i + 512], T.x[:, 512 * i:512 * i + 512], "dx%d" % i)
           for i in range(4)]
-    lw = load("s", T.wt[:], T.w[:], "dw", lx[0])
+    lw = load("s", T.wt[:], T.w[:], "dw", lx[2])
 
     iota = lambda out, pat, cm, base=0: done("g", g.iota(out, pat, base, cm, allow_small_or_imprecise_dtypes=True))
     k_u = fill(T.ut[:, 64:576], 0.0)
@@ -171,14 +172,16 @@ def rank_program(g, core, T, topo):
     iota(T.k16[:], [[0, 2], [1, 16]], 0)
     iota(T.kr[:], [[-1, 32]], 0, base=128)
     k_pm = iota(T.pm[:], [[32, 4], [128, 4], [16, 2]], 0)
-    k_g = iota(T.wvt[:, 128:192], [[0, 64]], 0)
+    iota(T.bs[:, 80:96], [[0, 16]], 0)
+    iota(T.c2[:], [[0, 64]], 0)
+    k_g = iota(T.wvt[:, 128:160], [[0, 32]], 0)
     qz = [quant(T.vq[:, i:i + 128], T.vs[:, i:i + 128], T.ut[:, 64:576], k_u) for i in (0, 160)]
     k_jn = ts(T.jn[:], T.jp[:], T.rc[:, 3:4], A.subtract, k_jp, k_rc)
     ts(T.rc[:, 1:2], T.rc[:, 3:4], 1.0 / 32, A.mult)
-    ts(T.rc[:, 2:3], T.rc[:, 3:4], 64.0, A.is_ge)
     k_nq = fill(T.nq[:], -0.25)
     fill(T.z32[:], 0.0)
     fill(T.low[:], -BIG)
+    ts(T.nj[:], T.jn[:], -1.0, A.mult, k_jn)
 
     qu = quant(T.uq[:], T.us[:], T.ut[:, 0:512], lu, k_u)
     q32 = T.jn[:, 0:1]
@@ -192,24 +195,24 @@ def rank_program(g, core, T, topo):
         c = slice(128 * i, 128 * i + 128)
         qx.append(quant(T.xq[:, c], T.xs[:, c], T.xt[:, 512 * i:512 * i + 512], lx[i]))
     first = [None, None]
-    for i in range(4):
+    for i, k in ((0, 0), (0, 1), (1, 0), (1, 1), (2, 0), (3, 0), (2, 1), (3, 1)):
         c, h = slice(128 * i, 128 * i + 128), slice(128 - 32 * i, 256 - 32 * i)
-        for k in range(2):
-            first[k] = mm(T.ps[:, 512 * k:512 * k + 128], T.vq[:, h], T.vs[:, h], T.xq[:, c], T.xs[:, c], u1, u2, qz, qx[i],
-                          start=i == 0, stop=i == 3)
+        first[k] = mm(T.ps[:, 512 * k:512 * k + 128], T.vq[:, h], T.vs[:, h], T.xq[:, c], T.xs[:, c], u1, u2, qz, qx[i],
+                      start=i == 0, stop=i == 3)
     tb = [turn(T.B[:, 0:128], T.ps[:, 0:128], first[0], k_con)] * 4
     tq = first[1]
     k_po = ts(T.po[:], T.pm[:], q32, A.add, k_pm, s2=T.rc[:, 0:1], op1=A.add)
-    load("s", T.mq[:, 0:64].bitcast(dt.uint8), T.xq[:, 0:64].bitcast(dt.uint8), "dpad", qx[0])
-    load("s", T.ms[:, 0:64], T.xs[:, 0:64], "dpad")
+    load("s", T.mq[:, 0:96].bitcast(dt.uint8), T.xq[:, 0:96].bitcast(dt.uint8), "dpad", qx[3])
+    load("s", T.ms[:, 0:96], T.xs[:, 0:96], "dpad")
     pad = ("dpad", 32)
     y_todo = []
     y_out = []
-    qw = perm = sc = neg = tie = bank_free = None
+    qw = perm = sc = neg = tie = bank_free = r3 = None
 
     def mask(b, c):
         k = 128 * b + 32 * c
-        return act(T.bm[:, k:k + 32], T.mb[:, 32:64] if c == 3 else T.mb[:, 0:32], IDENT, tb[c], k_con, bias=T.B[:, k:k + 1])
+        m = T.mb[:, 32:64] if c == 3 and b == 0 else T.mb[:, 0:32]
+        return act(T.bm[:, k:k + 32], m, IDENT, tb[c], k_con, bias=T.B[:, k:k + 1])
 
     for b in range(R):
         o = 128 * b
@@ -217,72 +220,79 @@ def rank_program(g, core, T, topo):
         sv = [T.B[:, o + 32 * c:o + 32 * c + 1] for c in range(4)]
         cm = lambda i, n: T.cmp[:, 640 * b + i:640 * b + i + n]
         qv = lambda i, n: T.Q[:, o + i:o + i + n] if b else T.ps[:, i:i + n]
-        qa = T.Q[:, o:o + 128] if b else T.ps[:, 512:640]
+        qa = lambda i, n: T.Q[:, o + i:o + i + n] if b else T.ps[:, 512 + i:512 + i + n]
         bm = lambda c: T.bm[:, o + 32 * c:o + 32 * c + 32]
+        eq = lambda c, *d: tt(cm(160 * c + 128, 32), qv(32 * c, 32), bm(c), A.is_equal, tie[c], *d)
+        ge = lambda c: ts(cm(160 * c, 32 * c), qv(0, 32 * c), sv[c], A.is_ge, tb[c])
+        gt = lambda c: ts(cm(160 * c + 32 * c, 128 - 32 * c), qv(32 * c, 128 - 32 * c), sv[c], A.is_gt)
+        nb = T.ns[:, b:b + 1]
         if b > 0:
-            turn(T.Q[:, o:o + 96], T.B[:, o:o + 96], tb[0:3])
-            tq = turn(T.Q[:, o + 96:o + 128], T.B[:, o + 96:o + 128], tb[3])
-            tie[3] = mask(b, 3)
+            e0 = eq(0, tq[0])
+            tq[3] = turn(T.Q[:, o + 96:o + 128], T.B[:, o + 96:o + 128], tb[3])
+            s0 = [act(cm(0, 96), qa(0, 96), SIGN, tq[2], neg, bias=nb), act(cm(96, 32), qa(96, 32), SIGN, tq[3], bias=nb)]
+            d1 = [ge(1), eq(1, tq[1])]
+            d2 = [ge(2), eq(2, tq[2])]
+            d3 = [ge(3), eq(3, tq[3]), gt(3)]
+            d1.append(gt(1))
+            d2.append(gt(2))
+            sums, runs = ((0, [s0, e0], 0),), ((3, d3), (1, d1), (2, d2))
         else:
-            neg = act(T.ns[:, 0:1], sv[0], COPY, tb[0], scale=-1.0)
+            neg = ts(nb, sv[0], -1.0, A.mult, tb)
             tie = [None] * 4
             tie[3], tie[0] = mask(b, 3), mask(b, 0)
             for c in (1, 2):
                 tie[c] = ts(bm(c), T.mb[:, 0:32], sv[c], A.add, tb)
-        s3 = act(cm(480, 128), qa, SIGN, tq, tb, scale=-1.0, bias=sv[3])
-        s0 = act(cm(0, 128), qa, SIGN, neg, bias=T.ns[:, b:b + 1])
-        tv = tq if b else tb
-        eq = lambda c: tt(cm(160 * c + 128, 32), qv(32 * c, 32), bm(c), A.is_equal, tv, tie[c])
-        cmpv = lambda c: [ts(cm(160 * c, 32 * c), qv(0, 32 * c), sv[c], A.is_ge, tv, tb),
-                          ts(cm(160 * c + 32 * c, 128 - 32 * c), qv(32 * c, 128 - 32 * c), sv[c], A.is_gt)]
-        if b > 0:
-            e0, e3 = eq(0), eq(3)
-            d1 = cmpv(1) + [eq(1)]
-            d2 = cmpv(2) + [eq(2)]
-        else:
-            d1, d2 = cmpv(1), cmpv(2)
+            s3 = act(cm(480, 128), qa(0, 128), SIGN, tq, tb, scale=-1.0, bias=sv[3])
+            s0 = act(cm(0, 128), qa(0, 128), SIGN, neg, bias=nb)
+            d1, d2 = [ge(1), gt(1)], [ge(2), gt(2)]
             e3, e0 = eq(3), eq(0)
             d1.append(eq(1))
             d2.append(eq(2))
             bank_free = [d1, d2, s0]
+            sums, runs = ((3, [s3, e3], 160), (0, [s0, e0], 0)), ((1, d1), (2, d2))
         l0 = 320 * b
-        lc = [T.ls[:, l0 + k:l0 + k + 1] for k in (79, 159, 239, 318)]
-        kk = [T.ki[:]] * 3 + [T.kr[:]]
+        lc = [T.ls[:, l0 + k:l0 + k + 1] for k in (79, 159, 239, 319 if b else 318)]
+        kk = [T.ki[:]] * 3 + [T.ki[:] if b else T.kr[:]]
         lr = [None] * 4
-        for c, d, k in ((3, [s3, e3], 160), (0, [s0, e0], 0)):
+        for c, d, k in sums:
             lr[c] = act(T.junk[:, l0 + k:l0 + k + 160], cm(160 * c, 160), RELU, d, accum_out=lc[c])
-        for c, d in ((1, d1), (2, d2)):
+        for c, d in runs:
             lr[c] = scan(T.ls[:, l0 + 80 * c:l0 + 80 * c + 80], cm(160 * c, 80), cm(160 * c + 80, 80), 0.0, A.add, d)
         cc = [slice(o + 32 * c, o + 32 * c + 32) for c in range(4)]
         wv = [ts(T.wv[:, cc[c]], kk[c], lc[c], A.is_equal, lr[c], k_g, s2=sv[c], op1=A.mult)
-              for c in ((3, 1, 0, 2) if b else (3, 1, 2, 0))]
-        wj = [ts(T.wj[:, cc[c]], kk[c], lc[c], A.is_equal, s2=T.jn[:, c:c + 1], op1=A.mult) for c in range(4)]
-        y0, z0, v32, b4 = 96 * b, 48 * b, slice(32 * b, 32 * b + 32), slice(4 * b, 4 * b + 4)
-        t2 = turn(T.wvt[:, 0:128], T.wv[:, o:o + 128], wv)
+              for c in ((3, 0, 1, 2) if b else (3, 1, 2, 0))]
+        ab = [act(T.ab[:, cc[c]], kk[c], ABS, lr[c], k_g, scale=-1.0, bias=lc[c]) for c in range(4)]
+        wj = [act(T.wj[:, cc[c]], T.ab[:, cc[c]], RELU, ab[c], scale=T.nj[:, c:c + 1], bias=T.jn[:, c:c + 1]) for c in range(4)]
+        for fn in y_todo:
+            y_out = fn()
+        y_todo = []
+        v0, v32, b4 = 64 * b, slice(32 * b, 32 * b + 32), slice(4 * b, 4 * b + 4)
+        i, k = (0, 64) if b else (64, 0)
+        turn(T.wvt[:, i:i + 64], T.wv[:, o + i:o + i + 64], wv[0:3])
+        t2 = turn(T.wvt[:, k:k + 64], T.wv[:, o + k:o + k + 64], wv)
+        if b == 0:
+            r3 = ts(T.ls[:, l0 + 319:l0 + 320], lc[3], -1.0, A.mult, s2=128.0, op1=A.add)
+        bs = scan(T.bs[:, 0:80], T.wvt[:, 0:160:2], T.wvt[:, 1:160:2], 0.0, A.add, t2)
         tj = turn(T.wjt[:, o:o + 128], T.wj[:, o:o + 128], wj)
         jcol = act(T.jj[:, o:o + 128], T.wjt[:, o:o + 128], IDENT, tj, bias=T.rc[:, 1:2], accum_out=T.jcol[:, b:b + 1])
-        if more:
-            r3 = ts(T.ls[:, l0 + 319:l0 + 320], lc[3], -1.0, A.mult, s2=128.0, op1=A.add)
-        bs = scan(T.bs[:, y0:y0 + 96], T.wvt[:, 0:192:2], T.wvt[:, 1:192:2], 0.0, A.add, t2)
+        t3 = turn(T.vt[:, v0:v0 + 32], T.bs[:, 64:96], bs)
+        t5 = [turn(T.vt[span(h, 2), v0 + 32:v0 + 64], T.bs[span(2 - h, 2), 64:96]) for h in (0, 2)]
+
+        row = lambda a, n=16, k=1: T.vt[span(a, k), v0:v0 + n]
+        vc = lambda a, k=1: T.bs[span(a, k), 79:80]
+        f = [ts(T.c2[span(0, 2), 0:16], row(2, 16, 2), vc(0, 2), A.is_gt, t3),
+             ts(T.c2[span(2, 2), 0:16], row(0, 16, 2), vc(2, 2), A.is_ge),
+             ts(T.c2[span(1), 16:32], row(0), vc(1), A.is_ge), ts(T.c2[span(2), 16:32], row(3), vc(2), A.is_gt),
+             ts(T.c2[span(1), 32:48], row(2), vc(1), A.is_gt), ts(T.c2[span(2), 32:48], row(1), vc(2), A.is_ge),
+             ts(T.c2[span(0), 16:64], row(1, 48), vc(0), A.is_gt, t5), ts(T.c2[span(3), 16:64], row(2, 48), vc(3), A.is_ge)]
         if b == 0:
             sc = vcopy(T.sc[:, 0:4], T.B[:, 0:128:32])
         else:
-            m1 = ts(T.m25[:, 4 * b - 4:4 * b], T.mx[:, 256 * b - 256 + 63:256 * b:64], -0.25, A.mult)
-        t3 = turn(T.vt[:, v32], T.bs[:, y0 + 64:y0 + 96], bs)
-
-        row = lambda p: T.vt[p, 32 * b:32 * b + 16]
-        vc = lambda p: T.bs[p, y0 + 95:y0 + 96]
-        c2 = lambda p, k: T.c2[p, z0 + 16 * k:z0 + 16 * k + 16]
-        sx = [act(c2(span(a), 2), row(span(a ^ 3)), SIGN, t3, scale=-1.0, bias=vc(span(a))) for a in range(3)]
-        f = [ts(c2(span(0, 2), 0), row(span(2, 2)), vc(span(0, 2)), A.is_gt, t3),
-             ts(c2(span(2, 2), 0), row(span(0, 2)), vc(span(2, 2)), A.is_ge)]
-        f += [ts(c2(span(a), 1), row(span(a ^ 1)), vc(span(a)), A.is_ge if a % 2 else A.is_gt) for a in range(4)]
-        f.append(ts(c2(span(3), 2), row(span(0)), vc(span(3)), A.is_ge))
-        f.append(ts(c2(span(0, 3), 2), c2(span(0, 3), 2), T.rc[span(0, 3), 2:3], A.is_lt, sx))
+            m1 = ts(T.m25[:, 4 * b - 4:4 * b], T.mx[:, 384 * b - 384 + 95:384 * b:96], -0.25, A.mult)
+        n2 = scan(T.n2[:, v32], T.c2[:, 0:32], T.c2[:, 32:64], q32, A.add, f)
         if b > 0:
             sc = tt(T.sc[:, b4], T.sc[:, 4 * b - 4:4 * b], T.m25[:, 4 * b - 4:4 * b], A.add, m1, sc)
-        n2 = scan(T.n2[:, 32 * b:32 * b + 24], T.c2[:, z0:z0 + 24], T.c2[:, z0 + 24:z0 + 48], q32, A.add, f)
-        nc, tc = T.n2[:, 32 * b + 23:32 * b + 24], T.tt[:, b:b + 1]
+        nc, tc = T.n2[:, 32 * b + 31:32 * b + 32], T.tt[:, b:b + 1]
         w2 = ts(T.w2[:, v32], T.k16[:], nc, A.is_equal, n2, jcol, s2=T.jcol[:, b:b + 1], op1=A.mult)
         if more:
             i1 = ts(T.ind[:, v32], T.z32[:], nc, A.add, s2=16.0, op1=A.is_lt)
@@ -295,30 +305,43 @@ def rank_program(g, core, T, topo):
         hc = lambda a: T.hh[span(a), 32 * b + 31:32 * b + 32]
         of = T["of%d" % b]
         oo = [ts(of[span(a), 0:1], hc(0), hc(1), A.add, hh) for a in range(4)]
-        l1 = ts(T.lb[span(0), v32], T.z32[span(0), :], hc(0), A.add, s2=hc(1), op1=A.add)
         if more:
             i4 = ts(T.pen[:, b4], T.ls[:, l0 + 79:l0 + 320:80], tc, A.is_lt, i3, r3, s2=-BIG, op1=A.mult)
-        m0 = col0(b, rank) + 16 * me
+        mine = 16 * me
+        m0 = col0(b, rank, at) + mine
         pk = vcopy(T.mq[:, m0:m0 + 16].bitcast(dt.uint32), T.xq[:].bitcast(dt.uint32).indirect(of[:, 0:1]), oo, qx)
         pz = act(T.ms[:, m0:m0 + 16], T.xs[:].indirect(of[:, 0:1]), COPY, oo, qx)
 
-        fe, fl = "fe%d" % b, "fl%d" % b
-        arr_q, arr_z = ("nq%d" % b, len(near_eng)), ("nz%d" % b, len(near_eng))
-        wait("g", [pk])
-        send(codes, b, 16 * me, 16, (mate, near_eng, arr_q[0]), (ahead, far_eng, fe))
-        wait("g", [pz])
-        send(plane, b, 16 * me, 16, (mate, near_eng, arr_z[0]), (ahead, far_eng, fe))
-        wait("g", [arr_q])
-        send(codes, b, 0, 32, (rest, far_eng, fl))
-        wait("g", [arr_z])
-        send(plane, b, 0, 32, (rest, far_eng, fl))
-        early = [arr_q, arr_z, (fe, n_early), pk, pz]
-        ready = early + [(fl, n_late)]
+        got = lambda name, n: ("%s%d" % (name, b), n)
+        if me == 0:
+            wait("g", [pz])
+            send(plane, b, at, mine, 16, (mate, near_eng, "nz"))
+            wait("g", [pk])
+            send(codes, b, at, mine, 16, (mate, near_eng, "nq"), ([cx[1], cy[1]], far_eng, "fq"))
+            send(plane, b, at, mine, 16, (cx, far_eng, "fz"))
+            wait("g", [got("nq", nn)])
+            send(codes, b, at, 0, 32, (cz, far_eng, "fz"))
+            wait("g", [got("nz", nn)])
+            send(plane, b, at, 0, 32, (cy[0:1], far_eng, "fz"))
+            far = got("fw", nn)
+        else:
+            wait("g", [pk])
+            send(codes, b, at, mine, 16, (mate, near_eng, "nq"), ([cx[1], cy[1]], far_eng, "fq"))
+            wait("g", [pz])
+            send(plane, b, at, mine, 16, (mate, near_eng, "nz"), (cx, far_eng, "fz"))
+            wait("g", [got("nz", nn)])
+            send(plane, b, at, 0, 32, (cz + cy[1:2], far_eng, "fz"))
+            far = got("fq", 4 * nf)
+            wait("g", [far])
+            send(codes, b, (at + 2) % nch, 0, 64, (mate, near_eng, "fw"))
+        early = [got("nq", nn), got("nz", nn), pk, pz]
+        ready = early + [far, got("fz", 5 * nf)]
 
-        l2 = turn(T.lt[span(0), v32], T.lb[span(0), v32], l1)
-        load("s", T.ch[b:b + 1, :], T.lt[0:1, 32 * b:32 * b + 16], "dch%d" % b, l2)
+        l1 = ts(T.lb[span(0), v32], T.z32[span(0), :], hc(0), A.add, s2=hc(1), op1=A.add)
         if more:
             sm = tt(T.sm[:, b4], T.B[:, o:o + 128:32], T.pen[:, b4], A.add, i4)
+        l2 = turn(T.lt[span(0), v32], T.lb[span(0), v32], l1)
+        load("s", T.ch[b:b + 1, :], T.lt[0:1, 32 * b:32 * b + 16], "dch%d" % b, l2)
         if b == 0:
             p1 = vcopy(T.pq[:].bitcast(dt.uint32), T.xq[:].bitcast(dt.uint32).indirect(T.po[:]), k_po)
             p2 = act(T.pz[:], T.xs[:].indirect(T.po[:]), COPY, k_po, qx)
@@ -329,50 +352,48 @@ def rank_program(g, core, T, topo):
             e = turn(T.sr[:], T.sb[:], e)
             for a in range(4):
                 load("s", T.se[0:1, 128 * a:128 * a + 128], T.sr[32 * a:32 * a + 1, :], "dse", e)
-        for fn in y_todo:
-            y_out = fn()
-        y_todo = []
 
-        n0 = 64 + 128 * b
+        n0 = 96 + 128 * b
         mq, ms = T.mq[:, n0:n0 + 128], T.ms[:, n0:n0 + 128]
         re_ = []
         if more:
             piece = lambda c: (T.pq[:, 128 * c:128 * c + 128], T.pz[:, 128 * c:128 * c + 128])
-            te = [mm(T.pe[:, 512 * c:512 * c + 128], *piece(c), T.mq[:, n0 - 64:n0 + 64], T.ms[:, n0 - 64:n0 + 64],
+            te = [mm(T.pe[:, 512 * c:512 * c + 128], *piece(c), T.mq[:, n0 - 96:n0 + 32], T.ms[:, n0 - 96:n0 + 32],
                      early, perm, pad, y_out) for c in range(4)]
-            re_ = [red(T.me[:, 4 * b + c:4 * b + c + 1], T.pe[:, 512 * c + 64:512 * c + 128], A.max, te[c]) for c in range(4)]
+            re_ = [red(T.me[:, 4 * b + c:4 * b + c + 1], T.pe[:, 512 * c + 96:512 * c + 128], A.max, te[c]) for c in range(4)]
             tm = [mm(T.ps[:, 512 * c:512 * c + 128], *piece(c), mq, ms, ready, bank_free) for c in range(4)]
             n = 128 * (b + 1)
             rd, tb = [None] * 4, [None] * 4
+            blk = lambda c: turn(T.Q[:, n + 32 * c:n + 32 * c + 32], T.B[:, n + 32 * c:n + 32 * c + 32], tb[c])
             for c in range(4):
-                i, k = 4 * b + c, 256 * b + 64 * c
-                rd[c] = scan(T.mx[:, k:k + 64], T.ps[:, 512 * c + 64:512 * c + 128], T.low[:], T.me[:, i:i + 1], A.max,
+                i, k = 4 * b + c, 384 * b + 96 * c
+                rd[c] = scan(T.mx[:, k:k + 96], T.ps[:, 512 * c + 32:512 * c + 128], T.low[:], T.me[:, i:i + 1], A.max,
                              tm[c], re_[c])
-                out, m1, s1 = T.B[:, n + 32 * c:n + 32 * c + 32], T.mx[:, k + 63:k + 64], T.sm[:, i:i + 1]
+                out, m1, s1 = T.B[:, n + 32 * c:n + 32 * c + 32], T.mx[:, k + 95:k + 96], T.sm[:, i:i + 1]
                 if c < 3:
                     tb[c] = act(out, T.nq[:], IDENT, rd[c], sm, k_nq, scale=m1, bias=s1)
                 else:
+                    tq = [blk(0), None, None, None]
                     tb[c] = ts(out, T.nq[:], m1, A.mult, rd[c], sm, s2=s1, op1=A.add)
+                    tq[1], tq[2] = blk(1), blk(2)
+            tie[0], tie[1] = mask(b + 1, 0), mask(b + 1, 1)
             neg = act(T.ns[:, b + 1:b + 2], T.B[:, n:n + 1], COPY, tb[0], scale=-1.0)
-            tie = [mask(b + 1, c) for c in range(3)] + [None]
+            tie[2], tie[3] = mask(b + 1, 2), mask(b + 1, 3)
             bank_free = list(rd)
         ty = mm(T.pe[:, 1536:1664], T.wq[:], T.ws[:], mq, ms, ready, qw, re_, y_out)
 
         def put(b=b, ty=ty):
-            k = slice(128 * b, 128 * b + 128)
-            if b == R - 1:
-                t = [vcopy(T.yo[:, k], T.pe[:, 1536:1664], ty)]
-            else:
-                r = 32 * ((at - 1) % nch)
-                t = [act(T.yo[:, 128 * b + r:128 * b + 128], T.pe[:, 1536:1664 - r], COPY, ty)]
-                if r:
-                    t.append(act(T.yo[:, 128 * b:128 * b + r], T.pe[:, 1664 - r:1664], COPY, ty))
+            cp = vcopy if b == R - 1 else lambda out, in_, d: act(out, in_, COPY, d)
+            k, r = slice(128 * b, 128 * b + 128), 32 * at
+            t = [cp(T.yo[:, 128 * b + r:128 * b + 128], T.pe[:, 1536:1664 - r], ty)]
+            if r:
+                t.append(cp(T.yo[:, 128 * b:128 * b + r], T.pe[:, 1664 - r:1664], ty))
             load("s", T.y[:, k], T.yo[:, k], "dy%d" % b, t)
             return t
         y_todo.append(put)
     for fn in y_todo:
         fn()
 
-    last = [("loc", R * (2 * len(near_eng) + 4 * len(far_eng))), ("dse", 64)] + [("s" + q, count[q]) for q in count]
+    last = [("loc", count["loc"]), ("dse", 64)] + [("s" + q, count[q]) for q in "vatg"]
     last += [("dy%d" % b, 16) for b in range(R)] + [("dch%d" % b, 16) for b in range(R)]
     wait("g", last)

@@ -9,6 +9,8 @@ RELU = ActivationFunctionType.Relu
 SIGN = ActivationFunctionType.Sign
 A = AluOpType
 BIG = 1e29
+BLK = (0, 2, 1, 3)
+STEP = 1024.0
 
 
 def sb(n, d="float32"):
@@ -24,19 +26,20 @@ SCRATCH = {
     "vq": sb(288, F8), "vs": sb(288, U8),
     "mq": sb(96 + 128 * R, F8), "ms": sb(96 + 128 * R, U8),
     "jp": sb(4), "jn": sb(4), "nj": sb(4),
-    "rc": sb(4),
-    "ki": sb(32), "kr": sb(32), "k16": sb(32),
-    "mb": sb(64),
-    "pm": sb(32), "po": sb(32, "uint16"),
+    "rc": sb(8),
+    "mr": sb(128), "ki": sb(96), "kr": sb(16),
+    "mb": sb(160),
+    "pm": sb(32), "pn": sb(32), "pp": sb(32), "po": sb(32, "uint16"),
     "zo": sb(2, "uint16"),
-    "nq": sb(32), "z32": sb(32), "low": sb(96),
-    "B": sb(128 * R),
+    "low": sb(96),
+    "B0": sb(128), "bm": sb(128),
+    "inn": sb(256 * R), "B": sb(256 * R),
     "Q": sb(128 * R),
-    "bm": sb(128 * R), "ns": sb(R), "cmp": sb(640 * R, BF), "junk": sb(320 * R, BF), "ls": sb(320 * R), "wv": sb(128 * R),
-    "ab": sb(128 * R), "wj": sb(128 * R, BF), "wvt": sb(160), "wjt": sb(128 * R, BF), "jj": sb(128 * R), "jcol": sb(R),
-    "bs": sb(96), "vt": sb(64 * R), "c2": sb(64, BF), "n2": sb(32 * R), "w2": sb(32 * R), "w2t": sb(32 * R), "hh": sb(32 * R),
-    "lb": sb(32 * R), "lt": sb(32 * R), "ind": sb(32 * R), "indt": sb(32 * R), "tt": sb(R), "pen": sb(4 * R),
-    "sm": sb(4 * R), "me": sb(4 * R), "mx": sb(384 * R), "m25": sb(4 * R), "sc": sb(4 * R), "sb": sb(128), "sr": sb(128),
+    "ns": sb(1), "cmp": sb(640 * R, BF), "junk": sb(320 * R, BF), "ls": sb(320 * R), "lf": sb(4 * R), "wv": sb(128 * R),
+    "wj": sb(128 * R, BF), "wvt": sb(192), "wjt": sb(128 * R, BF), "jj": sb(64 * R),
+    "bs": sb(96), "vt": sb(32 * R), "c2": sb(128, BF), "n2": sb(64 * R), "w2t": sb(32 * R), "hh": sb(R),
+    "lb": sb(32 * R), "lt": sb(32 * R), "ind": sb(32 * R), "tt": sb(2 * R), "pen": sb(4 * R),
+    "me": sb(4 * R), "mx": sb(384 * R), "sc": sb(4 * R), "sb": sb(128), "sr": sb(128),
     "yo": sb(512), "ps": ("psum", [128, 2048], "float32"), "pe": ("psum", [128, 2048], "float32"),
 }
 for _b in range(R):
@@ -52,28 +55,41 @@ def mask_of(engines):
 
 
 def rank_program(g, core, T, topo):
-    rank = T.rank_of(core)
-    if rank is None:
-        return
     cores = list(T.cores)
     chips = []
     for c in cores:
         if topo.chip(c) not in chips:
             chips.append(topo.chip(c))
-    nch = len(chips)
-    on = lambda ch: [r for r in range(len(cores)) if topo.chip(cores[r]) == ch]
-    place = lambda r: chips.index(topo.chip(cores[r]))
-    at = place(rank)
-    pair = on(chips[at])
-    me = pair.index(rank)
-    mate = [r for r in pair if r != rank]
-    cx, cy, cz = [on(chips[(at + k) % nch]) for k in (1, 2, 3)]
-    far_eng = topo.engines(core, cores[cx[0]])
-    near_eng = [e for e in topo.engines(core, cores[mate[0]]) if e not in far_eng]
+    if core not in cores:
+        return
+    here = topo.chip(core)
+    on = lambda ch: [c for c in cores if topo.chip(c) == ch]
+
+    ahead = lambda ch, k: chips[(chips.index(ch) + k) % len(chips)]
+
+    def lineup(c):
+        return [ahead(topo.chip(c), k) for k in range(len(chips))]
+    pair = on(here)
+    cx, cy, cz = [on(ahead(here, k)) for k in (1, 2, 3)]
+    far_eng = topo.engines(core, cz[0])
+    near_eng = [e for e in topo.engines(pair[0], pair[1]) if e not in far_eng]
     nf, nn = len(far_eng), len(near_eng)
 
-    def col0(b, r, ch):
-        return 96 + 128 * b + 32 * ((ch - place(r)) % nch)
+    def col0(b, c, ch):
+        return 96 + 128 * b + 32 * lineup(c).index(ch)
+
+    def send(view, b, ch, off, n, *groups):
+        cut = lambda c: view(col0(b, c, ch) + off, col0(b, c, ch) + off + n)
+        g.remote_dma_fused([
+            RemoteDMATransfer(dst_ids=[DstId(rid=topo.addr(c)[0], pnc=topo.addr(c)[1]) for c in to],
+                              dma_engine_mask=mask_of(eng), remote_sem=T.sem["%s%d" % (arr, b)], srcs=[cut(core)],
+                              dsts=[cut(c) for c in to])
+            for to, eng, arr in groups], local_sem=T.sem.loc)
+        count["loc"] += sum(len(eng) for to, eng, arr in groups)
+    codes = lambda i, j: T.mq[:, i:j].bitcast(dt.uint8)
+    plane = lambda i, j: T.ms[:, i:j]
+    me = pair.index(core)
+    mate = [c for c in pair if c != core]
 
     Q = {"v": g.vector, "a": g.scalar, "t": g.tensor, "g": g, "s": g.sync}
     count = {"v": 0, "a": 0, "t": 0, "g": 0, "loc": 0}
@@ -108,9 +124,9 @@ def rank_program(g, core, T, topo):
         wait("v", deps)
         return done("v", g.vector.tensor_tensor(out, a, b, op))
 
-    def red(out, in_, op, *deps):
+    def red(out, in_, op, *deps, size=False):
         wait("v", deps)
-        return done("v", g.vector.tensor_reduce(out, in_, AxisListType.X, op))
+        return done("v", g.vector.tensor_reduce(out, in_, AxisListType.X, op, apply_absolute_value=size))
 
     def scan(out, d0, d1, first, op, *deps):
         wait("v", deps)
@@ -144,23 +160,14 @@ def rank_program(g, core, T, topo):
         Q[q].dma_start(out, in_).then_inc(T.sem[sem], 16)
         return (sem, 16)
 
-    def send(view, b, ch, off, n, *groups):
-        cut = lambda r: view(col0(b, r, ch) + off, col0(b, r, ch) + off + n)
-        g.remote_dma_fused([
-            RemoteDMATransfer(dst_ids=[DstId(rid=topo.addr(cores[r])[0], pnc=topo.addr(cores[r])[1]) for r in to],
-                              dma_engine_mask=mask_of(eng), remote_sem=T.sem["%s%d" % (arr, b)], srcs=[cut(rank)],
-                              dsts=[cut(r) for r in to])
-            for to, eng, arr in groups], local_sem=T.sem.loc)
-        count["loc"] += sum(len(eng) for to, eng, arr in groups)
-    codes = lambda i, j: T.mq[:, i:j].bitcast(dt.uint8)
-    plane = lambda i, j: T.ms[:, i:j]
-
     def span(a, n=1):
         return slice(32 * a, 32 * a + 32 * n)
+    lo, hi = span(0, 2), span(2, 2)
 
     lu = load("a", T.ut[:, 0:64], T.u[:, 0:64], "du")
-    lx = [load("s" if i % 2 == 0 else "a", T.xt[:, 512 * i:512 * i + 512], T.x[:, 512 * i:512 * i + 512], "dx%d" % i)
-          for i in range(4)]
+    lx = []
+    for i, (p0, p1) in enumerate(((0, 1), (1, 2), (2, 3), (3, 4))):
+        lx += [load("sa"[i % 2], T.xt[:, 512 * p0:512 * p1], T.x[:, 512 * p0:512 * p1], "dx%d" % i)] * (p1 - p0)
     lw = load("s", T.wt[:], T.w[:], "dw", lx[2])
 
     iota = lambda out, pat, cm, base=0: done("g", g.iota(out, pat, base, cm, allow_small_or_imprecise_dtypes=True))
@@ -168,190 +175,218 @@ def rank_program(g, core, T, topo):
     k_rc = [fill(T.rc[span(a), 3:4], 32.0 * a) for a in range(4)]
     k_zo = fill(T.zo[:], 0)
     k_jp = iota(T.jp[:], [[32, 4]], 1)
-    k_ki = iota(T.ki[:], [[1, 32]], 0)
-    iota(T.k16[:], [[0, 2], [1, 16]], 0)
-    iota(T.kr[:], [[-1, 32]], 0, base=128)
-    k_pm = iota(T.pm[:], [[32, 4], [128, 4], [16, 2]], 0)
-    iota(T.bs[:, 80:96], [[0, 16]], 0)
-    iota(T.c2[:], [[0, 64]], 0)
-    k_g = iota(T.wvt[:, 128:160], [[0, 32]], 0)
-    qz = [quant(T.vq[:, i:i + 128], T.vs[:, i:i + 128], T.ut[:, 64:576], k_u) for i in (0, 160)]
-    k_jn = ts(T.jn[:], T.jp[:], T.rc[:, 3:4], A.subtract, k_jp, k_rc)
-    ts(T.rc[:, 1:2], T.rc[:, 3:4], 1.0 / 32, A.mult)
-    k_nq = fill(T.nq[:], -0.25)
-    fill(T.z32[:], 0.0)
+    k_ki = iota(T.ki[:], [[0, 3], [1, 32]], 0)
+    iota(T.mb[:, 32:64], [[0, 32]], 0)
+    k_z = iota(T.mb[:, 96:128], [[0, 32]], 0)
+    iota(T.wvt[:, 128:192], [[0, 64]], 0)
+    iota(T.kr[:], [[-1, 16]], 0, base=128)
+    iota(T.c2[:, 33:48], [[0, 15]], 0, base=-int(STEP))
+    iota(T.c2[:, 48:49], [[0, 1]], 0, base=15 * int(STEP))
+    iota(T.c2[:, 49:64], [[0, 15]], 0, base=-int(STEP))
+    k_g = iota(T.c2[:, 96:128], [[0, 32]], 0)
+    iota(T.pm[:], [[32, 4], [128, 2], [16, 4]], 0)
+    k_pm = iota(T.pn[:], [[0, 8], [224, 2], [0, 2]], 0)
+    z32 = lambda s=slice(0, 128): T.mb[s, 32:64]
     fill(T.low[:], -BIG)
-    ts(T.nj[:], T.jn[:], -1.0, A.mult, k_jn)
+    k_jn = ts(T.jn[:], T.jp[:], T.rc[:, 3:4], A.subtract, k_jp, k_rc)
+    qz = [quant(T.vq[:, i:i + 128], T.vs[:, i:i + 128], T.ut[:, 64:576], k_u) for i in (0, 160)]
+    q32 = T.jn[:, 0:1]
+    col = lambda i, s=slice(0, 128): T.rc[s, i:i + 1]
+    k32 = T.ki[:, 0:32]
+    k_r0 = ts(col(0), q32, 16.0, A.is_ge, k_jn, s2=-16.0, op1=A.mult)
+    ts(col(4), q32, 16.0, A.is_lt, s2=STEP, op1=A.mult)
+    ts(col(5), q32, 16.0, A.is_ge, s2=STEP, op1=A.mult)
 
     qu = quant(T.uq[:], T.us[:], T.ut[:, 0:512], lu, k_u)
-    q32 = T.jn[:, 0:1]
-    ts(T.mb[:, 0:32], T.ki[:], q32, A.is_ge, k_ki, k_jn, s2=BIG, op1=A.mult)
-    ts(T.mb[:, 32:64], T.ki[:], q32, A.is_lt, s2=BIG, op1=A.mult)
-    k_con = ts(T.rc[:, 0:1], q32, 16.0, A.is_ge, s2=-16.0, op1=A.mult)
-    u1 = vcopy(T.vq[:, 128:160].bitcast(dt.uint32), T.uq[:].bitcast(dt.uint32).indirect(T.zo[:, 0:2]), qu, k_zo)
     u2 = act(T.vs[:, 128:160], T.us[:].indirect(T.zo[:, 0:2]), COPY, qu, k_zo)
     qx = []
     for i in range(4):
         c = slice(128 * i, 128 * i + 128)
         qx.append(quant(T.xq[:, c], T.xs[:, c], T.xt[:, 512 * i:512 * i + 512], lx[i]))
+        if i == 0:
+            u1 = vcopy(T.vq[:, 128:160].bitcast(dt.uint32), T.uq[:].bitcast(dt.uint32).indirect(T.zo[:, 0:2]), qu, k_zo)
+    ts(T.mr[:, 0:96], T.ki[:], q32, A.is_ge, k_ki, s2=-BIG, op1=A.mult)
+    k_mr = ts(T.mr[:, 96:128], k32, q32, A.is_lt, s2=-BIG, op1=A.mult)
+    k_r2 = ts(col(2), q32, col(0), A.add, k_r0)
+    ts(T.mb[:, 0:32], k32, q32, A.is_ge, s2=-BIG, op1=A.mult)
+    ts(T.mb[:, 64:96], k32, q32, A.is_ge, s2=-BIG, op1=A.mult)
+    ts(T.mb[:, 128:160], k32, q32, A.is_lt, s2=-BIG, op1=A.mult)
     first = [None, None]
-    for i, k in ((0, 0), (0, 1), (1, 0), (1, 1), (2, 0), (3, 0), (2, 1), (3, 1)):
-        c, h = slice(128 * i, 128 * i + 128), slice(128 - 32 * i, 256 - 32 * i)
+    for i, k in [(i, k) for k in (0, 1) for i in range(4)]:
+        c, h = slice(128 * i, 128 * i + 128), slice(128 - 32 * BLK[i], 256 - 32 * BLK[i])
         first[k] = mm(T.ps[:, 512 * k:512 * k + 128], T.vq[:, h], T.vs[:, h], T.xq[:, c], T.xs[:, c], u1, u2, qz, qx[i],
                       start=i == 0, stop=i == 3)
-    tb = [turn(T.B[:, 0:128], T.ps[:, 0:128], first[0], k_con)] * 4
+    tb = [None] * 4
+    tb[3] = turn(T.B0[:, 96:128], T.ps[:, 96:128], first[0], k_mr)
+    tb[0] = turn(T.B0[:, 0:32], T.ps[:, 0:32])
+    hide = lambda i, n: tt(T.bm[:, i:i + n], T.ps[:, i:i + n], T.mr[:, i:i + n], A.add)
+    tie = [hide(96, 32), hide(0, 32)]
+    tb[1] = tb[2] = turn(T.B0[:, 32:96], T.ps[:, 32:96])
+    tie.append(hide(32, 64))
+    k_r7 = ts(col(7), T.jp[:, 0:1], col(2), A.subtract, k_r2, s2=128.0 / 16, op1=A.mult)
+    ts(col(6), col(2), -STEP, A.mult, s2=16 * STEP, op1=A.add)
     tq = first[1]
-    k_po = ts(T.po[:], T.pm[:], q32, A.add, k_pm, s2=T.rc[:, 0:1], op1=A.add)
     load("s", T.mq[:, 0:96].bitcast(dt.uint8), T.xq[:, 0:96].bitcast(dt.uint8), "dpad", qx[3])
     load("s", T.ms[:, 0:96], T.xs[:, 0:96], "dpad")
     pad = ("dpad", 32)
     y_todo = []
     y_out = []
-    qw = perm = sc = neg = tie = bank_free = r3 = None
-
-    def mask(b, c):
-        k = 128 * b + 32 * c
-        m = T.mb[:, 32:64] if c == 3 and b == 0 else T.mb[:, 0:32]
-        return act(T.bm[:, k:k + 32], m, IDENT, tb[c], k_con, bias=T.B[:, k:k + 1])
+    qw = perm = sc = bank_free = None
+    AT_B, AT_M = (32, 64, 160, 192), (0, 96, 128, 224)
+    masks = (T.mb[:, 0:64], T.mb[:, 32:96], T.mb[:, 0:64], T.mb[:, 96:160])
 
     for b in range(R):
         o = 128 * b
         more = b < R - 1
-        sv = [T.B[:, o + 32 * c:o + 32 * c + 1] for c in range(4)]
+        GT, GE, LT = (A.is_lt, A.is_le, A.is_gt) if b else (A.is_gt, A.is_ge, A.is_lt)
+        one = lambda at, s=slice(0, 128): at[0][s, at[1]:at[1] + 1]
+        sat = [(T.B, 2 * o + AT_B[c]) if b else (T.B0, 32 * c) for c in range(4)]
+        sv = [one(a) for a in sat]
         cm = lambda i, n: T.cmp[:, 640 * b + i:640 * b + i + n]
         qv = lambda i, n: T.Q[:, o + i:o + i + n] if b else T.ps[:, i:i + n]
         qa = lambda i, n: T.Q[:, o + i:o + i + n] if b else T.ps[:, 512 + i:512 + i + n]
-        bm = lambda c: T.bm[:, o + 32 * c:o + 32 * c + 32]
-        eq = lambda c, *d: tt(cm(160 * c + 128, 32), qv(32 * c, 32), bm(c), A.is_equal, tie[c], *d)
-        ge = lambda c: ts(cm(160 * c, 32 * c), qv(0, 32 * c), sv[c], A.is_ge, tb[c])
-        gt = lambda c: ts(cm(160 * c + 32 * c, 128 - 32 * c), qv(32 * c, 128 - 32 * c), sv[c], A.is_gt)
-        nb = T.ns[:, b:b + 1]
+        bm = lambda c: T.B[:, 2 * o + AT_M[c]:2 * o + AT_M[c] + 32] if b else T.bm[:, 32 * c:32 * c + 32]
+        eq = lambda c, *d: tt(cm(160 * c + 128, 32), qv(32 * c, 32), bm(c), A.is_equal, *d)
+        ge = lambda c, *d: ts(cm(160 * c, 32 * c), qv(0, 32 * c), sv[c], GE, *d)
+        gt = lambda c, *d: ts(cm(160 * c + 32 * c, 128 - 32 * c), qv(32 * c, 128 - 32 * c), sv[c], GT, *d)
+        l0 = 320 * b
+        lat = [(T.lf, 4 * b), (T.ls, l0 + 159), (T.ls, l0 + 239), (T.ls, l0 + 319) if b else (T.lf, 3)]
+        lc = [one(a) for a in lat]
+        lr = [None] * 4
+        relu = lambda c, d, k=1.0: act(T.junk[:, l0 + 160 * (c // 3):l0 + 160 * (c // 3) + 160], cm(160 * c, 160), RELU, d,
+                                       scale=k, accum_out=lc[c])
+        run = lambda c, d: scan(T.ls[:, l0 + 80 * c:l0 + 80 * c + 80], cm(160 * c, 80), cm(160 * c + 80, 80), 0.0, A.add, d)
         if b > 0:
+            blk = lambda c, d: turn(qv(32 * c, 32), T.B[:, 2 * o + AT_B[c]:2 * o + AT_B[c] + 32], d)
+            gp = lambda c, i, n, *d: ts(cm(160 * c + i, n), qv(i, n), sv[c], GT if c < 3 else LT, *d)
+            tq = [blk(c, tb[c]) for c in range(4)]
+            s3 = act(cm(480, 64), qa(0, 64), SIGN, tq[1], scale=-1.0, bias=sv[3])
+            s0 = [act(cm(0, 96), qa(0, 96), SIGN, tq[2], scale=-1.0, bias=sv[0]),
+                  act(cm(96, 32), qa(96, 32), SIGN, tq[3], scale=-1.0, bias=sv[0])]
             e0 = eq(0, tq[0])
-            tq[3] = turn(T.Q[:, o + 96:o + 128], T.B[:, o + 96:o + 128], tb[3])
-            s0 = [act(cm(0, 96), qa(0, 96), SIGN, tq[2], neg, bias=nb), act(cm(96, 32), qa(96, 32), SIGN, tq[3], bias=nb)]
             d1 = [ge(1), eq(1, tq[1])]
             d2 = [ge(2), eq(2, tq[2])]
-            d3 = [ge(3), eq(3, tq[3]), gt(3)]
-            d1.append(gt(1))
-            d2.append(gt(2))
-            sums, runs = ((0, [s0, e0], 0),), ((3, d3), (1, d1), (2, d2))
+            d1.append(gp(1, 32, 96, tq[3]))
+            d2.append(gp(2, 64, 64))
+            d3 = [gp(3, 64, 64), eq(3)]
+            part = T.lf[:, 4 * b + 3:4 * b + 4]
+            d3.append(act(T.junk[:, l0 + 160:l0 + 224], cm(480, 64), RELU, s3, scale=-1.0, accum_out=part))
+            lr[0] = relu(0, [s0, e0])
+            lr[1], lr[2] = run(1, d1), run(2, d2)
+            lr[3] = scan(T.ls[:, l0 + 272:l0 + 320], cm(544, 48), cm(592, 48), part, A.add, d3)
         else:
-            neg = ts(nb, sv[0], -1.0, A.mult, tb)
-            tie = [None] * 4
-            tie[3], tie[0] = mask(b, 3), mask(b, 0)
-            for c in (1, 2):
-                tie[c] = ts(bm(c), T.mb[:, 0:32], sv[c], A.add, tb)
-            s3 = act(cm(480, 128), qa(0, 128), SIGN, tq, tb, scale=-1.0, bias=sv[3])
-            s0 = act(cm(0, 128), qa(0, 128), SIGN, neg, bias=nb)
-            d1, d2 = [ge(1), gt(1)], [ge(2), gt(2)]
-            e3, e0 = eq(3), eq(0)
-            d1.append(eq(1))
-            d2.append(eq(2))
+            eq = lambda c, k, *d: ts(cm(160 * c + 128, 32), bm(c), sv[c], A.is_equal, *d, s2=k, op1=A.mult)
+            s3 = act(cm(480, 128), qa(0, 128), SIGN, tq, tb[3], scale=-1.0, bias=sv[3])
+            s0 = act(cm(0, 128), qa(0, 128), SIGN, tb[0], scale=-1.0, bias=sv[0])
+            e3, e0 = eq(3, 1.0, tie[0]), eq(0, -1.0, tie[1])
+            d1 = [ge(1, tb[1]), gt(1), eq(1, 1.0, tie)]
+            d2 = [ge(2), gt(2), eq(2, 1.0)]
             bank_free = [d1, d2, s0]
-            sums, runs = ((3, [s3, e3], 160), (0, [s0, e0], 0)), ((1, d1), (2, d2))
-        l0 = 320 * b
-        lc = [T.ls[:, l0 + k:l0 + k + 1] for k in (79, 159, 239, 319 if b else 318)]
-        kk = [T.ki[:]] * 3 + [T.ki[:] if b else T.kr[:]]
-        lr = [None] * 4
-        for c, d, k in sums:
-            lr[c] = act(T.junk[:, l0 + k:l0 + k + 160], cm(160 * c, 160), RELU, d, accum_out=lc[c])
-        for c, d in runs:
-            lr[c] = scan(T.ls[:, l0 + 80 * c:l0 + 80 * c + 80], cm(160 * c, 80), cm(160 * c + 80, 80), 0.0, A.add, d)
+            lr[3], lr[0] = relu(3, [s3, e3]), relu(0, [s0, e0], -1.0)
+            lr[1], lr[2] = run(1, d1), run(2, d2)
+        kk = [T.ki] * 3 + [T.kr]
         cc = [slice(o + 32 * c, o + 32 * c + 32) for c in range(4)]
-        wv = [ts(T.wv[:, cc[c]], kk[c], lc[c], A.is_equal, lr[c], k_g, s2=sv[c], op1=A.mult)
-              for c in ((3, 0, 1, 2) if b else (3, 1, 2, 0))]
-        ab = [act(T.ab[:, cc[c]], kk[c], ABS, lr[c], k_g, scale=-1.0, bias=lc[c]) for c in range(4)]
-        wj = [act(T.wj[:, cc[c]], T.ab[:, cc[c]], RELU, ab[c], scale=T.nj[:, c:c + 1], bias=T.jn[:, c:c + 1]) for c in range(4)]
+        order = (1, 2, 0, 3) if b else (1, 2, 3, 0)
         for fn in y_todo:
             y_out = fn()
         y_todo = []
-        v0, v32, b4 = 64 * b, slice(32 * b, 32 * b + 32), slice(4 * b, 4 * b + 4)
-        i, k = (0, 64) if b else (64, 0)
-        turn(T.wvt[:, i:i + 64], T.wv[:, o + i:o + i + 64], wv[0:3])
-        t2 = turn(T.wvt[:, k:k + 64], T.wv[:, o + k:o + k + 64], wv)
-        if b == 0:
-            r3 = ts(T.ls[:, l0 + 319:l0 + 320], lc[3], -1.0, A.mult, s2=128.0, op1=A.add)
-        bs = scan(T.bs[:, 0:80], T.wvt[:, 0:160:2], T.wvt[:, 1:160:2], 0.0, A.add, t2)
-        tj = turn(T.wjt[:, o:o + 128], T.wj[:, o:o + 128], wj)
-        jcol = act(T.jj[:, o:o + 128], T.wjt[:, o:o + 128], IDENT, tj, bias=T.rc[:, 1:2], accum_out=T.jcol[:, b:b + 1])
-        t3 = turn(T.vt[:, v0:v0 + 32], T.bs[:, 64:96], bs)
-        t5 = [turn(T.vt[span(h, 2), v0 + 32:v0 + 64], T.bs[span(2 - h, 2), 64:96]) for h in (0, 2)]
-
-        row = lambda a, n=16, k=1: T.vt[span(a, k), v0:v0 + n]
-        vc = lambda a, k=1: T.bs[span(a, k), 79:80]
-        f = [ts(T.c2[span(0, 2), 0:16], row(2, 16, 2), vc(0, 2), A.is_gt, t3),
-             ts(T.c2[span(2, 2), 0:16], row(0, 16, 2), vc(2, 2), A.is_ge),
-             ts(T.c2[span(1), 16:32], row(0), vc(1), A.is_ge), ts(T.c2[span(2), 16:32], row(3), vc(2), A.is_gt),
-             ts(T.c2[span(1), 32:48], row(2), vc(1), A.is_gt), ts(T.c2[span(2), 32:48], row(1), vc(2), A.is_ge),
-             ts(T.c2[span(0), 16:64], row(1, 48), vc(0), A.is_gt, t5), ts(T.c2[span(3), 16:64], row(2, 48), vc(3), A.is_ge)]
-        if b == 0:
-            sc = vcopy(T.sc[:, 0:4], T.B[:, 0:128:32])
-        else:
-            m1 = ts(T.m25[:, 4 * b - 4:4 * b], T.mx[:, 384 * b - 384 + 95:384 * b:96], -0.25, A.mult)
-        n2 = scan(T.n2[:, v32], T.c2[:, 0:32], T.c2[:, 32:64], q32, A.add, f)
+        def hot(out, c, at, *d):
+            for h, s in enumerate((lo, hi)):
+                k = o + 32 * c + 16 * h
+                t = ts(out[lo, k:k + 16], kk[c][s, 0:16], one(lat[c], s), A.is_equal, *d, s2=one(at, s), op1=A.mult)
+            return t
+        num = lambda two: [hot(T.wj, c, (T.jn, c)) for c in two]
+        wv = [hot(T.wv, c, sat[c], lr[c], k_g) for c in order[0:2]]
+        wj = num(order[0:2])
+        wv += [hot(T.wv, c, sat[c], lr[c]) for c in order[2:4]]
+        v32, b4 = slice(32 * b, 32 * b + 32), slice(4 * b, 4 * b + 4)
+        wj += num(order[2:4])
         if b > 0:
-            sc = tt(T.sc[:, b4], T.sc[:, 4 * b - 4:4 * b], T.m25[:, 4 * b - 4:4 * b], A.add, m1, sc)
-        nc, tc = T.n2[:, 32 * b + 31:32 * b + 32], T.tt[:, b:b + 1]
-        w2 = ts(T.w2[:, v32], T.k16[:], nc, A.is_equal, n2, jcol, s2=T.jcol[:, b:b + 1], op1=A.mult)
+            sc = tt(T.sc[:, b4], T.sc[:, 4 * b - 4:4 * b], T.mx[:, 384 * b - 384 + 95:384 * b:96], A.add, sc)
+        else:
+            sc = ts(T.sc[:, 0:4], T.B0[:, 0:128:32], -4.0, A.mult)
+            ts(T.c2[:, 0:1], col(2), STEP, A.mult, k_r7, s2=col(7), op1=A.add)
+        turn(T.wvt[lo, 32:96], T.wv[lo, o + 32:o + 96], wv[0:2])
+        t2 = [turn(T.wvt[lo, 32 * c:32 * c + 32], T.wv[lo, cc[c]], d) for c, d in zip(order[2:4], wv[2:4])]
+        tj = turn(T.wjt[lo, o:o + 128], T.wj[lo, o:o + 128], wj)
+        if not more:
+            e = [ts(T.sb[:, 32 * c:32 * c + 32], z32(), T.sc[:, 4 * b + c:4 * b + c + 1], A.add, sc, s2=-0.25, op1=A.mult)
+                 for c in range(4)]
+        bs = scan(T.bs[lo, 1:96], T.wvt[lo, 0:190:2], T.wvt[lo, 1:190:2], 0.0, A.add, t2)
+        jc = T.jj[lo, 64 * b + 63:64 * b + 64]
+        jcol = scan(T.jj[lo, 64 * b:64 * b + 64], T.wjt[lo, o:o + 64], T.wjt[lo, o + 64:o + 128], 0.0, A.add, tj)
+        t3 = turn(T.vt[lo, v32], T.bs[lo, 64:96], bs)
+        row = lambda s, i, n: T.vt[s, 32 * b + i:32 * b + i + n]
+        vc = lambda s: T.bs[s, 64:65]
+        f = [ts(T.c2[lo, 1:17], row(lo, 16, 16), vc(lo), GT, t3, s2=col(4, lo), op1=A.mult),
+             ts(T.c2[lo, 17:33], row(lo, 0, 16), vc(lo), GE, s2=col(5, lo), op1=A.mult),
+             ts(T.c2[span(0), 64:96], row(span(1), 0, 32), vc(span(0)), GT, s2=STEP, op1=A.mult),
+             ts(T.c2[span(1), 64:96], row(span(0), 0, 32), vc(span(1)), GE, s2=STEP, op1=A.mult)]
+        if not more:
+            e = turn(T.sr[:], T.sb[:], e)
+            for a in range(4):
+                load("sa"[a % 2], T.se[0:1, 128 * BLK[a]:128 * BLK[a] + 128], T.sr[32 * a:32 * a + 1, :], "dse", e)
+        n2 = scan(T.n2[lo, 64 * b:64 * b + 64], T.c2[lo, 0:64], T.c2[lo, 64:128], jc, A.add, f, jcol)
+        t4 = turn(T.w2t[lo, v32], T.n2[lo, 64 * b + 32:64 * b + 64], n2)
+        hh = red(T.hh[lo, b:b + 1], T.w2t[lo, v32], A.min, t4, size=True)
         if more:
-            i1 = ts(T.ind[:, v32], T.z32[:], nc, A.add, s2=16.0, op1=A.is_lt)
-        t4 = turn(T.w2t[:, v32], T.w2[:, v32], w2)
-        if more:
-            i2 = turn(T.indt[:, v32], T.ind[:, v32], i1)
-        hh = scan(T.hh[span(0, 2), v32], T.w2t[span(0, 2), v32], T.w2t[span(2, 2), v32], 0.0, A.add, t4)
-        if more:
-            i3 = red(tc, T.indt[:, v32], A.add, i2)
-        hc = lambda a: T.hh[span(a), 32 * b + 31:32 * b + 32]
+            i1 = ts(T.ind[lo, v32], T.w2t[lo, v32], col(6, lo), A.is_lt)
+        hc = lambda a: T.hh[span(a), b:b + 1]
         of = T["of%d" % b]
-        oo = [ts(of[span(a), 0:1], hc(0), hc(1), A.add, hh) for a in range(4)]
-        if more:
-            i4 = ts(T.pen[:, b4], T.ls[:, l0 + 79:l0 + 320:80], tc, A.is_lt, i3, r3, s2=-BIG, op1=A.mult)
+        oo = [ts(of[span(a), 0:1], hc(0), hc(1), A.min, hh) for a in range(4)]
+        l1 = ts(T.lb[span(0), v32], z32(span(0)), hc(0), A.add, k_z, s2=hc(1), op1=A.min)
         mine = 16 * me
-        m0 = col0(b, rank, at) + mine
+        m0 = col0(b, core, here) + mine
         pk = vcopy(T.mq[:, m0:m0 + 16].bitcast(dt.uint32), T.xq[:].bitcast(dt.uint32).indirect(of[:, 0:1]), oo, qx)
         pz = act(T.ms[:, m0:m0 + 16], T.xs[:].indirect(of[:, 0:1]), COPY, oo, qx)
 
         got = lambda name, n: ("%s%d" % (name, b), n)
+        soon = [cx[1], cy[1]]
         if me == 0:
-            wait("g", [pz])
-            send(plane, b, at, mine, 16, (mate, near_eng, "nz"))
             wait("g", [pk])
-            send(codes, b, at, mine, 16, (mate, near_eng, "nq"), ([cx[1], cy[1]], far_eng, "fq"))
-            send(plane, b, at, mine, 16, (cx, far_eng, "fz"))
+            send(codes, b, here, mine, 16, (soon, far_eng, "fq"))
+            wait("g", [pz])
+            send(plane, b, here, mine, 16, (mate, near_eng, "nz"), (cx, far_eng, "fz"))
+            send(codes, b, here, mine, 16, (mate, near_eng, "nq"))
             wait("g", [got("nq", nn)])
-            send(codes, b, at, 0, 32, (cz, far_eng, "fz"))
+            send(codes, b, here, 0, 32, (cz, far_eng, "fz"))
             wait("g", [got("nz", nn)])
-            send(plane, b, at, 0, 32, (cy[0:1], far_eng, "fz"))
+            send(plane, b, here, 0, 32, (cy[0:1], far_eng, "fz"))
             far = got("fw", nn)
         else:
             wait("g", [pk])
-            send(codes, b, at, mine, 16, (mate, near_eng, "nq"), ([cx[1], cy[1]], far_eng, "fq"))
+            send(codes, b, here, mine, 16, (mate, near_eng, "nq"), (soon, far_eng, "fq"))
             wait("g", [pz])
-            send(plane, b, at, mine, 16, (mate, near_eng, "nz"), (cx, far_eng, "fz"))
+            send(plane, b, here, mine, 16, (mate, near_eng, "nz"), (cx, far_eng, "fz"))
             wait("g", [got("nz", nn)])
-            send(plane, b, at, 0, 32, (cz + cy[1:2], far_eng, "fz"))
+            send(plane, b, here, 0, 32, (cz + cy[1:2], far_eng, "fz"))
             far = got("fq", 4 * nf)
             wait("g", [far])
-            send(codes, b, (at + 2) % nch, 0, 64, (mate, near_eng, "fw"))
+            send(codes, b, topo.chip(cy[0]), 0, 64, (mate, near_eng, "fw"))
         early = [got("nq", nn), got("nz", nn), pk, pz]
         ready = early + [far, got("fz", 5 * nf)]
 
-        l1 = ts(T.lb[span(0), v32], T.z32[span(0), :], hc(0), A.add, s2=hc(1), op1=A.add)
-        if more:
-            sm = tt(T.sm[:, b4], T.B[:, o:o + 128:32], T.pen[:, b4], A.add, i4)
-        l2 = turn(T.lt[span(0), v32], T.lb[span(0), v32], l1)
-        load("s", T.ch[b:b + 1, :], T.lt[0:1, 32 * b:32 * b + 16], "dch%d" % b, l2)
         if b == 0:
+            k_pp = tt(T.pp[:], T.pm[:], T.pn[:], A.add, k_pm)
+        l2 = turn(T.lt[span(0), v32], T.lb[span(0), v32], l1)
+        load("s", T.ch[b:b + 1, :], T.lt[0:1, 32 * b:32 * b + 16], "dch%d" % b, l2, ready)
+        if b == 0:
+            k_po = ts(T.po[:], T.pp[:], col(2), A.add, k_pp)
             p1 = vcopy(T.pq[:].bitcast(dt.uint32), T.xq[:].bitcast(dt.uint32).indirect(T.po[:]), k_po)
             p2 = act(T.pz[:], T.xs[:].indirect(T.po[:]), COPY, k_po, qx)
             perm = [p1, p2]
+        if more:
+            tc, td = T.tt[:, 2 * b:2 * b + 1], T.tt[:, 2 * b + 1:2 * b + 2]
+            i3 = [red(T.tt[span(a), 2 * b:2 * b + 1], T.ind[span(a % 2), 32 * b + 16 * (a // 2):32 * b + 16 * (a // 2) + 16],
+                      A.add, i1) for a in range(4)]
+            i4 = ts(td, tc, -1.0, A.mult, i3, s2=128.0, op1=A.add)
+            i5 = [ts(T.pen[:, 4 * b + c:4 * b + c + 1], lc[c], tc, A.is_lt, s2=BIG, op1=A.mult) for c in range(3)]
+            i5.append(ts(T.pen[:, 4 * b + 3:4 * b + 4], lc[3], td, A.is_gt, i4, s2=BIG, op1=A.mult))
+            inn = [T.inn[:, 2 * o + 64 * c:2 * o + 64 * c + 64] for c in range(4)]
+            sm = [ts(inn[c], masks[c], sv[c] if b else T.sc[:, c:c + 1], A.add, i5, sc,
+                     s2=T.pen[:, 4 * b + c:4 * b + c + 1], op1=A.add) for c in range(4)]
+        if b == 0:
             qw = quant(T.wq[:], T.ws[:], T.wt[:], lw)
-        if not more:
-            e = [ts(T.sb[:, 32 * c:32 * c + 32], T.z32[:], T.sc[:, 4 * b + c:4 * b + c + 1], A.add, sc) for c in range(4)]
-            e = turn(T.sr[:], T.sb[:], e)
-            for a in range(4):
-                load("s", T.se[0:1, 128 * a:128 * a + 128], T.sr[32 * a:32 * a + 1, :], "dse", e)
 
         n0 = 96 + 128 * b
         mq, ms = T.mq[:, n0:n0 + 128], T.ms[:, n0:n0 + 128]
@@ -363,31 +398,30 @@ def rank_program(g, core, T, topo):
             re_ = [red(T.me[:, 4 * b + c:4 * b + c + 1], T.pe[:, 512 * c + 96:512 * c + 128], A.max, te[c]) for c in range(4)]
             tm = [mm(T.ps[:, 512 * c:512 * c + 128], *piece(c), mq, ms, ready, bank_free) for c in range(4)]
             n = 128 * (b + 1)
-            rd, tb = [None] * 4, [None] * 4
-            blk = lambda c: turn(T.Q[:, n + 32 * c:n + 32 * c + 32], T.B[:, n + 32 * c:n + 32 * c + 32], tb[c])
+            rd, tb, tq = [None] * 4, [None] * 4, [None] * 4
             for c in range(4):
                 i, k = 4 * b + c, 384 * b + 96 * c
                 rd[c] = scan(T.mx[:, k:k + 96], T.ps[:, 512 * c + 32:512 * c + 128], T.low[:], T.me[:, i:i + 1], A.max,
                              tm[c], re_[c])
-                out, m1, s1 = T.B[:, n + 32 * c:n + 32 * c + 32], T.mx[:, k + 95:k + 96], T.sm[:, i:i + 1]
-                if c < 3:
-                    tb[c] = act(out, T.nq[:], IDENT, rd[c], sm, k_nq, scale=m1, bias=s1)
-                else:
-                    tq = [blk(0), None, None, None]
-                    tb[c] = ts(out, T.nq[:], m1, A.mult, rd[c], sm, s2=s1, op1=A.add)
-                    tq[1], tq[2] = blk(1), blk(2)
-            tie[0], tie[1] = mask(b + 1, 0), mask(b + 1, 1)
-            neg = act(T.ns[:, b + 1:b + 2], T.B[:, n:n + 1], COPY, tb[0], scale=-1.0)
-            tie[2], tie[3] = mask(b + 1, 2), mask(b + 1, 3)
+
+            for c, i, w in ((0, 0, 64), (1, 64, 64), (2, 128, 64), (3, 192, 32), (3, 224, 32)):
+                k = 384 * b + 96 * c + 95
+                t = ts(T.B[:, 2 * n + i:2 * n + i + w], T.inn[:, 2 * o + i:2 * o + i + w], T.mx[:, k:k + 1], A.add, rd[c], sm)
+                tb[c] = tb[c] or t
             bank_free = list(rd)
         ty = mm(T.pe[:, 1536:1664], T.wq[:], T.ws[:], mq, ms, ready, qw, re_, y_out)
 
         def put(b=b, ty=ty):
             cp = vcopy if b == R - 1 else lambda out, in_, d: act(out, in_, COPY, d)
-            k, r = slice(128 * b, 128 * b + 128), 32 * at
-            t = [cp(T.yo[:, 128 * b + r:128 * b + 128], T.pe[:, 1536:1664 - r], ty)]
-            if r:
-                t.append(cp(T.yo[:, 128 * b:128 * b + r], T.pe[:, 1664 - r:1664], ty))
+            k, t, i = slice(128 * b, 128 * b + 128), [], 0
+            to = [chips.index(ch) for ch in lineup(core)]
+            while i < 4:
+                n = 1
+                while i + n < 4 and to[i + n] == to[i] + n:
+                    n += 1
+                j = 128 * b + 32 * to[i]
+                t.append(cp(T.yo[:, j:j + 32 * n], T.pe[:, 1536 + 32 * i:1536 + 32 * (i + n)], ty))
+                i += n
             load("s", T.y[:, k], T.yo[:, k], "dy%d" % b, t)
             return t
         y_todo.append(put)

from concourse.bass import DstId, RemoteDMATransfer
from concourse.mybir import dt, AluOpType, AxisListType, ActivationFunctionType

R = 4
COPY = ActivationFunctionType.Copy
IDENT = ActivationFunctionType.Identity
ABS = ActivationFunctionType.Abs
RELU = ActivationFunctionType.Relu
SIGN = ActivationFunctionType.Sign
A = AluOpType
BIG = 1e29
BLK = (0, 2, 1, 3)
STEP = 1024.0


def sb(n, d="float32"):
    return ("sbuf", [128, n], d)


F8, U8, BF = "float8_e4m3fn_x4", "uint8", "bfloat16"
SCRATCH = {
    "xt": sb(2048, BF), "ut": sb(576, BF), "wt": sb(512, BF),
    "xq": sb(512, F8), "xs": sb(512, U8),
    "pq": sb(512, F8), "pz": sb(512, U8),
    "uq": sb(128, F8), "us": sb(128, U8), "wq": sb(128, F8), "ws": sb(128, U8),
    "vq": sb(288, F8), "vs": sb(288, U8),
    "mq": sb(96 + 128 * R, F8), "ms": sb(96 + 128 * R, U8),
    "jp": sb(4), "jn": sb(4), "nj": sb(4),
    "rc": sb(8),
    "mr": sb(128), "ki": sb(96), "kr": sb(16),
    "mb": sb(160),
    "pm": sb(32), "pn": sb(32), "pp": sb(32), "po": sb(32, "uint16"),
    "zo": sb(2, "uint16"),
    "low": sb(96),
    "B0": sb(128), "bm": sb(128),
    "inn": sb(256 * R), "B": sb(256 * R),
    "Q": sb(128 * R),
    "ns": sb(1), "cmp": sb(640 * R, BF), "junk": sb(320 * R, BF), "ls": sb(320 * R), "lf": sb(4 * R), "wv": sb(128 * R),
    "wj": sb(128 * R, BF), "wvt": sb(192), "wjt": sb(128 * R, BF), "jj": sb(64 * R),
    "bs": sb(96), "vt": sb(32 * R), "c2": sb(128, BF), "n2": sb(64 * R), "w2t": sb(32 * R), "hh": sb(R),
    "lb": sb(32 * R), "lt": sb(32 * R), "ind": sb(32 * R), "tt": sb(2 * R), "pen": sb(4 * R),
    "me": sb(4 * R), "mx": sb(384 * R), "sc": sb(4 * R), "sb": sb(128), "sr": sb(128),
    "yo": sb(512), "ps": ("psum", [128, 2048], "float32"), "pe": ("psum", [128, 2048], "float32"),
}
for _b in range(R):
    SCRATCH["of%d" % _b] = sb(2, "uint16")

SEMAPHORES = ["sv", "sa", "st", "sg", "du", "dw", "dse", "dpad", "loc"]
SEMAPHORES += ["dx%d" % i for i in range(4)]
SEMAPHORES += ["%s%d" % (n, b) for n in ("nq", "nz", "fq", "fz", "fw", "dy", "dch") for b in range(R)]


def mask_of(engines):
    return sum(1 << e for e in engines)


def rank_program(g, core, T, topo):
    cores = list(T.cores)
    chips = []
    for c in cores:
        if topo.chip(c) not in chips:
            chips.append(topo.chip(c))
    if core not in cores:
        return
    here = topo.chip(core)
    on = lambda ch: [c for c in cores if topo.chip(c) == ch]

    ahead = lambda ch, k: chips[(chips.index(ch) + k) % len(chips)]

    def lineup(c):
        return [ahead(topo.chip(c), k) for k in range(len(chips))]
    pair = on(here)
    cx, cy, cz = [on(ahead(here, k)) for k in (1, 2, 3)]
    far_eng = topo.engines(core, cz[0])
    near_eng = [e for e in topo.engines(pair[0], pair[1]) if e not in far_eng]
    nf, nn = len(far_eng), len(near_eng)

    def col0(b, c, ch):
        return 96 + 128 * b + 32 * lineup(c).index(ch)

    def send(view, b, ch, off, n, *groups):
        cut = lambda c: view(col0(b, c, ch) + off, col0(b, c, ch) + off + n)
        g.remote_dma_fused([
            RemoteDMATransfer(dst_ids=[DstId(rid=topo.addr(c)[0], pnc=topo.addr(c)[1]) for c in to],
                              dma_engine_mask=mask_of(eng), remote_sem=T.sem["%s%d" % (arr, b)], srcs=[cut(core)],
                              dsts=[cut(c) for c in to])
            for to, eng, arr in groups], local_sem=T.sem.loc)
        count["loc"] += sum(len(eng) for to, eng, arr in groups)
    codes = lambda i, j: T.mq[:, i:j].bitcast(dt.uint8)
    plane = lambda i, j: T.ms[:, i:j]
    me = pair.index(core)
    mate = [c for c in pair if c != core]

    Q = {"v": g.vector, "a": g.scalar, "t": g.tensor, "g": g, "s": g.sync}
    count = {"v": 0, "a": 0, "t": 0, "g": 0, "loc": 0}
    seen = {k: {} for k in Q}

    def flat(deps, need):
        for d in deps:
            if isinstance(d, list):
                flat(d, need)
            elif d is not None:
                need[d[0]] = max(need.get(d[0], 0), d[1])
        return need

    def wait(q, deps):
        for s, n in flat(deps, {}).items():
            if seen[q].get(s, 0) < n:
                Q[q].wait_ge(T.sem[s], n)
                seen[q][s] = n

    def done(q, ins):
        count[q] += 1
        ins.then_inc(T.sem["s" + q], 1)
        return ("s" + q, count[q])

    def ts(out, in0, s1, op0, *deps, s2=None, op1=None):
        wait("v", deps)
        if op1 is None:
            return done("v", g.vector.tensor_scalar(out, in0, s1, None, op0))
        return done("v", g.vector.tensor_scalar(out, in0, s1, s2, op0, op1))

    def tt(out, a, b, op, *deps):
        wait("v", deps)
        return done("v", g.vector.tensor_tensor(out, a, b, op))

    def red(out, in_, op, *deps, size=False):
        wait("v", deps)
        return done("v", g.vector.tensor_reduce(out, in_, AxisListType.X, op, apply_absolute_value=size))

    def scan(out, d0, d1, first, op, *deps):
        wait("v", deps)
        return done("v", g.vector.tensor_tensor_scan(out, d0, d1, first, op, op))

    def turn(out, in_, *deps):
        wait("v", deps)
        return done("v", g.vector.transpose(out, in_))

    def vcopy(out, in_, *deps):
        wait("v", deps)
        return done("v", g.vector.tensor_copy(out, in_))

    def fill(out, c):
        return done("v", g.vector.memset(out, c))

    def quant(q, s, x, *deps):
        wait("v", deps)
        return done("v", g.vector.quantize_mx(q, s, x))

    def act(out, in_, func, *deps, **kw):
        wait("a", deps)
        return done("a", g.scalar.activation(out, in_, func, **kw))

    def mm(out, lq, ls, rq, rs, *deps, start=True, stop=True):
        wait("t", deps)
        return done("t", g.tensor.matmul_mx(out, lq, ls, rq, rs, start, stop))

    def load(q, out, in_, sem, *deps):
        wait(q, deps)
        Q[q].dma_start(out, in_).then_inc(T.sem[sem], 16)
        return (sem, 16)

    def span(a, n=1):
        return slice(32 * a, 32 * a + 32 * n)
    lo, hi = span(0, 2), span(2, 2)

    lu = load("a", T.ut[:, 0:64], T.u[:, 0:64], "du")
    lx = []
    for i, (p0, p1) in enumerate(((0, 1), (1, 2), (2, 3), (3, 4))):
        lx += [load("sa"[i % 2], T.xt[:, 512 * p0:512 * p1], T.x[:, 512 * p0:512 * p1], "dx%d" % i)] * (p1 - p0)
    lw = load("s", T.wt[:], T.w[:], "dw", lx[2])

    iota = lambda out, pat, cm, base=0: done("g", g.iota(out, pat, base, cm, allow_small_or_imprecise_dtypes=True))
    k_u = fill(T.ut[:, 64:576], 0.0)
    k_rc = [fill(T.rc[span(a), 3:4], 32.0 * a) for a in range(4)]
    k_zo = fill(T.zo[:], 0)
    k_jp = iota(T.jp[:], [[32, 4]], 1)
    k_ki = iota(T.ki[:], [[0, 3], [1, 32]], 0)
    iota(T.mb[:, 32:64], [[0, 32]], 0)
    k_z = iota(T.mb[:, 96:128], [[0, 32]], 0)
    iota(T.wvt[:, 128:192], [[0, 64]], 0)
    iota(T.kr[:], [[-1, 16]], 0, base=128)
    iota(T.c2[:, 33:48], [[0, 15]], 0, base=-int(STEP))
    iota(T.c2[:, 48:49], [[0, 1]], 0, base=15 * int(STEP))
    iota(T.c2[:, 49:64], [[0, 15]], 0, base=-int(STEP))
    k_g = iota(T.c2[:, 96:128], [[0, 32]], 0)
    iota(T.pm[:], [[32, 4], [128, 2], [16, 4]], 0)
    k_pm = iota(T.pn[:], [[0, 8], [224, 2], [0, 2]], 0)
    z32 = lambda s=slice(0, 128): T.mb[s, 32:64]
    fill(T.low[:], -BIG)
    k_jn = ts(T.jn[:], T.jp[:], T.rc[:, 3:4], A.subtract, k_jp, k_rc)
    qz = [quant(T.vq[:, i:i + 128], T.vs[:, i:i + 128], T.ut[:, 64:576], k_u) for i in (0, 160)]
    q32 = T.jn[:, 0:1]
    col = lambda i, s=slice(0, 128): T.rc[s, i:i + 1]
    k32 = T.ki[:, 0:32]
    k_r0 = ts(col(0), q32, 16.0, A.is_ge, k_jn, s2=-16.0, op1=A.mult)
    ts(col(4), q32, 16.0, A.is_lt, s2=STEP, op1=A.mult)
    ts(col(5), q32, 16.0, A.is_ge, s2=STEP, op1=A.mult)

    qu = quant(T.uq[:], T.us[:], T.ut[:, 0:512], lu, k_u)
    u2 = act(T.vs[:, 128:160], T.us[:].indirect(T.zo[:, 0:2]), COPY, qu, k_zo)
    qx = []
    for i in range(4):
        c = slice(128 * i, 128 * i + 128)
        qx.append(quant(T.xq[:, c], T.xs[:, c], T.xt[:, 512 * i:512 * i + 512], lx[i]))
        if i == 0:
            u1 = vcopy(T.vq[:, 128:160].bitcast(dt.uint32), T.uq[:].bitcast(dt.uint32).indirect(T.zo[:, 0:2]), qu, k_zo)
    ts(T.mr[:, 0:96], T.ki[:], q32, A.is_ge, k_ki, s2=-BIG, op1=A.mult)
    k_mr = ts(T.mr[:, 96:128], k32, q32, A.is_lt, s2=-BIG, op1=A.mult)
    k_r2 = ts(col(2), q32, col(0), A.add, k_r0)
    ts(T.mb[:, 0:32], k32, q32, A.is_ge, s2=-BIG, op1=A.mult)
    ts(T.mb[:, 64:96], k32, q32, A.is_ge, s2=-BIG, op1=A.mult)
    ts(T.mb[:, 128:160], k32, q32, A.is_lt, s2=-BIG, op1=A.mult)
    first = [None, None]
    for i, k in [(i, k) for k in (0, 1) for i in range(4)]:
        c, h = slice(128 * i, 128 * i + 128), slice(128 - 32 * BLK[i], 256 - 32 * BLK[i])
        first[k] = mm(T.ps[:, 512 * k:512 * k + 128], T.vq[:, h], T.vs[:, h], T.xq[:, c], T.xs[:, c], u1, u2, qz, qx[i],
                      start=i == 0, stop=i == 3)
    tb = [None] * 4
    tb[3] = turn(T.B0[:, 96:128], T.ps[:, 96:128], first[0], k_mr)
    tb[0] = turn(T.B0[:, 0:32], T.ps[:, 0:32])
    hide = lambda i, n: tt(T.bm[:, i:i + n], T.ps[:, i:i + n], T.mr[:, i:i + n], A.add)
    tie = [hide(96, 32), hide(0, 32)]
    tb[1] = tb[2] = turn(T.B0[:, 32:96], T.ps[:, 32:96])
    tie.append(hide(32, 64))
    k_r7 = ts(col(7), T.jp[:, 0:1], col(2), A.subtract, k_r2, s2=128.0 / 16, op1=A.mult)
    ts(col(6), col(2), -STEP, A.mult, s2=16 * STEP, op1=A.add)
    tq = first[1]
    load("s", T.mq[:, 0:96].bitcast(dt.uint8), T.xq[:, 0:96].bitcast(dt.uint8), "dpad", qx[3])
    load("s", T.ms[:, 0:96], T.xs[:, 0:96], "dpad")
    pad = ("dpad", 32)
    y_todo = []
    y_out = []
    qw = perm = sc = bank_free = None
    AT_B, AT_M = (32, 64, 160, 192), (0, 96, 128, 224)
    masks = (T.mb[:, 0:64], T.mb[:, 32:96], T.mb[:, 0:64], T.mb[:, 96:160])

    for b in range(R):
        o = 128 * b
        more = b < R - 1
        GT, GE, LT = (A.is_lt, A.is_le, A.is_gt) if b else (A.is_gt, A.is_ge, A.is_lt)
        one = lambda at, s=slice(0, 128): at[0][s, at[1]:at[1] + 1]
        sat = [(T.B, 2 * o + AT_B[c]) if b else (T.B0, 32 * c) for c in range(4)]
        sv = [one(a) for a in sat]
        cm = lambda i, n: T.cmp[:, 640 * b + i:640 * b + i + n]
        qv = lambda i, n: T.Q[:, o + i:o + i + n] if b else T.ps[:, i:i + n]
        qa = lambda i, n: T.Q[:, o + i:o + i + n] if b else T.ps[:, 512 + i:512 + i + n]
        bm = lambda c: T.B[:, 2 * o + AT_M[c]:2 * o + AT_M[c] + 32] if b else T.bm[:, 32 * c:32 * c + 32]
        eq = lambda c, *d: tt(cm(160 * c + 128, 32), qv(32 * c, 32), bm(c), A.is_equal, *d)
        ge = lambda c, *d: ts(cm(160 * c, 32 * c), qv(0, 32 * c), sv[c], GE, *d)
        gt = lambda c, *d: ts(cm(160 * c + 32 * c, 128 - 32 * c), qv(32 * c, 128 - 32 * c), sv[c], GT, *d)
        l0 = 320 * b
        lat = [(T.lf, 4 * b), (T.ls, l0 + 159), (T.ls, l0 + 239), (T.ls, l0 + 319) if b else (T.lf, 3)]
        lc = [one(a) for a in lat]
        lr = [None] * 4
        relu = lambda c, d, k=1.0: act(T.junk[:, l0 + 160 * (c // 3):l0 + 160 * (c // 3) + 160], cm(160 * c, 160), RELU, d,
                                       scale=k, accum_out=lc[c])
        run = lambda c, d: scan(T.ls[:, l0 + 80 * c:l0 + 80 * c + 80], cm(160 * c, 80), cm(160 * c + 80, 80), 0.0, A.add, d)
        if b > 0:
            blk = lambda c, d: turn(qv(32 * c, 32), T.B[:, 2 * o + AT_B[c]:2 * o + AT_B[c] + 32], d)
            gp = lambda c, i, n, *d: ts(cm(160 * c + i, n), qv(i, n), sv[c], GT if c < 3 else LT, *d)
            tq = [blk(c, tb[c]) for c in range(4)]
            s3 = act(cm(480, 64), qa(0, 64), SIGN, tq[1], scale=-1.0, bias=sv[3])
            s0 = [act(cm(0, 96), qa(0, 96), SIGN, tq[2], scale=-1.0, bias=sv[0]),
                  act(cm(96, 32), qa(96, 32), SIGN, tq[3], scale=-1.0, bias=sv[0])]
            e0 = eq(0, tq[0])
            d1 = [ge(1), eq(1, tq[1])]
            d2 = [ge(2), eq(2, tq[2])]
            d1.append(gp(1, 32, 96, tq[3]))
            d2.append(gp(2, 64, 64))
            d3 = [gp(3, 64, 64), eq(3)]
            part = T.lf[:, 4 * b + 3:4 * b + 4]
            d3.append(act(T.junk[:, l0 + 160:l0 + 224], cm(480, 64), RELU, s3, scale=-1.0, accum_out=part))
            lr[0] = relu(0, [s0, e0])
            lr[1], lr[2] = run(1, d1), run(2, d2)
            lr[3] = scan(T.ls[:, l0 + 272:l0 + 320], cm(544, 48), cm(592, 48), part, A.add, d3)
        else:
            eq = lambda c, k, *d: ts(cm(160 * c + 128, 32), bm(c), sv[c], A.is_equal, *d, s2=k, op1=A.mult)
            s3 = act(cm(480, 128), qa(0, 128), SIGN, tq, tb[3], scale=-1.0, bias=sv[3])
            s0 = act(cm(0, 128), qa(0, 128), SIGN, tb[0], scale=-1.0, bias=sv[0])
            e3, e0 = eq(3, 1.0, tie[0]), eq(0, -1.0, tie[1])
            d1 = [ge(1, tb[1]), gt(1), eq(1, 1.0, tie)]
            d2 = [ge(2), gt(2), eq(2, 1.0)]
            bank_free = [d1, d2, s0]
            lr[3], lr[0] = relu(3, [s3, e3]), relu(0, [s0, e0], -1.0)
            lr[1], lr[2] = run(1, d1), run(2, d2)
        kk = [T.ki] * 3 + [T.kr]
        cc = [slice(o + 32 * c, o + 32 * c + 32) for c in range(4)]
        order = (1, 2, 0, 3) if b else (1, 2, 3, 0)
        for fn in y_todo:
            y_out = fn()
        y_todo = []
        def hot(out, c, at, *d):
            for h, s in enumerate((lo, hi)):
                k = o + 32 * c + 16 * h
                t = ts(out[lo, k:k + 16], kk[c][s, 0:16], one(lat[c], s), A.is_equal, *d, s2=one(at, s), op1=A.mult)
            return t
        num = lambda two: [hot(T.wj, c, (T.jn, c)) for c in two]
        wv = [hot(T.wv, c, sat[c], lr[c], k_g) for c in order[0:2]]
        wj = num(order[0:2])
        wv += [hot(T.wv, c, sat[c], lr[c]) for c in order[2:4]]
        v32, b4 = slice(32 * b, 32 * b + 32), slice(4 * b, 4 * b + 4)
        wj += num(order[2:4])
        if b > 0:
            sc = tt(T.sc[:, b4], T.sc[:, 4 * b - 4:4 * b], T.mx[:, 384 * b - 384 + 95:384 * b:96], A.add, sc)
        else:
            sc = ts(T.sc[:, 0:4], T.B0[:, 0:128:32], -4.0, A.mult)
            ts(T.c2[:, 0:1], col(2), STEP, A.mult, k_r7, s2=col(7), op1=A.add)
        turn(T.wvt[lo, 32:96], T.wv[lo, o + 32:o + 96], wv[0:2])
        t2 = [turn(T.wvt[lo, 32 * c:32 * c + 32], T.wv[lo, cc[c]], d) for c, d in zip(order[2:4], wv[2:4])]
        tj = turn(T.wjt[lo, o:o + 128], T.wj[lo, o:o + 128], wj)
        if not more:
            e = [ts(T.sb[:, 32 * c:32 * c + 32], z32(), T.sc[:, 4 * b + c:4 * b + c + 1], A.add, sc, s2=-0.25, op1=A.mult)
                 for c in range(4)]
        bs = scan(T.bs[lo, 1:96], T.wvt[lo, 0:190:2], T.wvt[lo, 1:190:2], 0.0, A.add, t2)
        jc = T.jj[lo, 64 * b + 63:64 * b + 64]
        jcol = scan(T.jj[lo, 64 * b:64 * b + 64], T.wjt[lo, o:o + 64], T.wjt[lo, o + 64:o + 128], 0.0, A.add, tj)
        t3 = turn(T.vt[lo, v32], T.bs[lo, 64:96], bs)
        row = lambda s, i, n: T.vt[s, 32 * b + i:32 * b + i + n]
        vc = lambda s: T.bs[s, 64:65]
        f = [ts(T.c2[lo, 1:17], row(lo, 16, 16), vc(lo), GT, t3, s2=col(4, lo), op1=A.mult),
             ts(T.c2[lo, 17:33], row(lo, 0, 16), vc(lo), GE, s2=col(5, lo), op1=A.mult),
             ts(T.c2[span(0), 64:96], row(span(1), 0, 32), vc(span(0)), GT, s2=STEP, op1=A.mult),
             ts(T.c2[span(1), 64:96], row(span(0), 0, 32), vc(span(1)), GE, s2=STEP, op1=A.mult)]
        if not more:
            e = turn(T.sr[:], T.sb[:], e)
            for a in range(4):
                load("sa"[a % 2], T.se[0:1, 128 * BLK[a]:128 * BLK[a] + 128], T.sr[32 * a:32 * a + 1, :], "dse", e)
        n2 = scan(T.n2[lo, 64 * b:64 * b + 64], T.c2[lo, 0:64], T.c2[lo, 64:128], jc, A.add, f, jcol)
        t4 = turn(T.w2t[lo, v32], T.n2[lo, 64 * b + 32:64 * b + 64], n2)
        hh = red(T.hh[lo, b:b + 1], T.w2t[lo, v32], A.min, t4, size=True)
        if more:
            i1 = ts(T.ind[lo, v32], T.w2t[lo, v32], col(6, lo), A.is_lt)
        hc = lambda a: T.hh[span(a), b:b + 1]
        of = T["of%d" % b]
        oo = [ts(of[span(a), 0:1], hc(0), hc(1), A.min, hh) for a in range(4)]
        l1 = ts(T.lb[span(0), v32], z32(span(0)), hc(0), A.add, k_z, s2=hc(1), op1=A.min)
        mine = 16 * me
        m0 = col0(b, core, here) + mine
        pk = vcopy(T.mq[:, m0:m0 + 16].bitcast(dt.uint32), T.xq[:].bitcast(dt.uint32).indirect(of[:, 0:1]), oo, qx)
        pz = act(T.ms[:, m0:m0 + 16], T.xs[:].indirect(of[:, 0:1]), COPY, oo, qx)

        got = lambda name, n: ("%s%d" % (name, b), n)
        soon = [cx[1], cy[1]]
        if me == 0:
            wait("g", [pk])
            send(codes, b, here, mine, 16, (soon, far_eng, "fq"))
            wait("g", [pz])
            send(plane, b, here, mine, 16, (mate, near_eng, "nz"), (cx, far_eng, "fz"))
            send(codes, b, here, mine, 16, (mate, near_eng, "nq"))
            wait("g", [got("nq", nn)])
            send(codes, b, here, 0, 32, (cz, far_eng, "fz"))
            wait("g", [got("nz", nn)])
            send(plane, b, here, 0, 32, (cy[0:1], far_eng, "fz"))
            far = got("fw", nn)
        else:
            wait("g", [pk])
            send(codes, b, here, mine, 16, (mate, near_eng, "nq"), (soon, far_eng, "fq"))
            wait("g", [pz])
            send(plane, b, here, mine, 16, (mate, near_eng, "nz"), (cx, far_eng, "fz"))
            wait("g", [got("nz", nn)])
            send(plane, b, here, 0, 32, (cz + cy[1:2], far_eng, "fz"))
            far = got("fq", 4 * nf)
            wait("g", [far])
            send(codes, b, topo.chip(cy[0]), 0, 64, (mate, near_eng, "fw"))
        early = [got("nq", nn), got("nz", nn), pk, pz]
        ready = early + [far, got("fz", 5 * nf)]

        if b == 0:
            k_pp = tt(T.pp[:], T.pm[:], T.pn[:], A.add, k_pm)
        l2 = turn(T.lt[span(0), v32], T.lb[span(0), v32], l1)
        load("s", T.ch[b:b + 1, :], T.lt[0:1, 32 * b:32 * b + 16], "dch%d" % b, l2, ready)
        if b == 0:
            k_po = ts(T.po[:], T.pp[:], col(2), A.add, k_pp)
            p1 = vcopy(T.pq[:].bitcast(dt.uint32), T.xq[:].bitcast(dt.uint32).indirect(T.po[:]), k_po)
            p2 = act(T.pz[:], T.xs[:].indirect(T.po[:]), COPY, k_po, qx)
            perm = [p1, p2]
        if more:
            tc, td = T.tt[:, 2 * b:2 * b + 1], T.tt[:, 2 * b + 1:2 * b + 2]
            i3 = [red(T.tt[span(a), 2 * b:2 * b + 1], T.ind[span(a % 2), 32 * b + 16 * (a // 2):32 * b + 16 * (a // 2) + 16],
                      A.add, i1) for a in range(4)]
            i4 = ts(td, tc, -1.0, A.mult, i3, s2=128.0, op1=A.add)
            i5 = [ts(T.pen[:, 4 * b + c:4 * b + c + 1], lc[c], tc, A.is_lt, s2=BIG, op1=A.mult) for c in range(3)]
            i5.append(ts(T.pen[:, 4 * b + 3:4 * b + 4], lc[3], td, A.is_gt, i4, s2=BIG, op1=A.mult))
            inn = [T.inn[:, 2 * o + 64 * c:2 * o + 64 * c + 64] for c in range(4)]
            sm = [ts(inn[c], masks[c], sv[c] if b else T.sc[:, c:c + 1], A.add, i5, sc,
                     s2=T.pen[:, 4 * b + c:4 * b + c + 1], op1=A.add) for c in range(4)]
        if b == 0:
            qw = quant(T.wq[:], T.ws[:], T.wt[:], lw)

        n0 = 96 + 128 * b
        mq, ms = T.mq[:, n0:n0 + 128], T.ms[:, n0:n0 + 128]
        re_ = []
        if more:
            piece = lambda c: (T.pq[:, 128 * c:128 * c + 128], T.pz[:, 128 * c:128 * c + 128])
            te = [mm(T.pe[:, 512 * c:512 * c + 128], *piece(c), T.mq[:, n0 - 96:n0 + 32], T.ms[:, n0 - 96:n0 + 32],
                     early, perm, pad, y_out) for c in range(4)]
            re_ = [red(T.me[:, 4 * b + c:4 * b + c + 1], T.pe[:, 512 * c + 96:512 * c + 128], A.max, te[c]) for c in range(4)]
            tm = [mm(T.ps[:, 512 * c:512 * c + 128], *piece(c), mq, ms, ready, bank_free) for c in range(4)]
            n = 128 * (b + 1)
            rd, tb, tq = [None] * 4, [None] * 4, [None] * 4
            for c in range(4):
                i, k = 4 * b + c, 384 * b + 96 * c
                rd[c] = scan(T.mx[:, k:k + 96], T.ps[:, 512 * c + 32:512 * c + 128], T.low[:], T.me[:, i:i + 1], A.max,
                             tm[c], re_[c])

            for c, i, w in ((0, 0, 64), (1, 64, 64), (2, 128, 64), (3, 192, 32), (3, 224, 32)):
                k = 384 * b + 96 * c + 95
                t = ts(T.B[:, 2 * n + i:2 * n + i + w], T.inn[:, 2 * o + i:2 * o + i + w], T.mx[:, k:k + 1], A.add, rd[c], sm)
                tb[c] = tb[c] or t
            bank_free = list(rd)
        ty = mm(T.pe[:, 1536:1664], T.wq[:], T.ws[:], mq, ms, ready, qw, re_, y_out)

        def put(b=b, ty=ty):
            cp = vcopy if b == R - 1 else lambda out, in_, d: act(out, in_, COPY, d)
            k, t, i = slice(128 * b, 128 * b + 128), [], 0
            to = [chips.index(ch) for ch in lineup(core)]
            while i < 4:
                n = 1
                while i + n < 4 and to[i + n] == to[i] + n:
                    n += 1
                j = 128 * b + 32 * to[i]
                t.append(cp(T.yo[:, j:j + 32 * n], T.pe[:, 1536 + 32 * i:1536 + 32 * (i + n)], ty))
                i += n
            load("s", T.y[:, k], T.yo[:, k], "dy%d" % b, t)
            return t
        y_todo.append(put)
    for fn in y_todo:
        fn()

    last = [("loc", count["loc"]), ("dse", 64)] + [("s" + q, count[q]) for q in "vatg"]
    last += [("dy%d" % b, 16) for b in range(R)] + [("dch%d" % b, 16) for b in range(R)]
    wait("g", last)
